import numpy as np
import ml_dtypes


def mxq(x, axis, fmt="e4m3"):
    dtype, down = {"e4m3": (ml_dtypes.float8_e4m3fn, 7), "e5m2": (ml_dtypes.float8_e5m2, 14)}[fmt]
    v = np.moveaxis(np.asarray(x, np.float32).astype(ml_dtypes.bfloat16).astype(np.float64), axis, -1)
    blocks = v.reshape(v.shape[:-1] + (-1, 32))
    amax = np.abs(blocks).max(-1, keepdims=True)
    byte = np.maximum(np.where(amax > 0, np.frexp(amax)[1] - 1 + 127, 0) - down, 1)
    scale = np.exp2(byte - 127.0)
    codes = (blocks / scale).astype(np.float32).astype(dtype).astype(np.float64)
    return np.moveaxis((codes * scale).reshape(v.shape), -1, axis)


WIDE = False


def mx_kscale(k):
    if not WIDE:
        return np.ones(k)
    levels = np.array([10, -10, 5, -5, 0])
    if k % 512:
        return np.exp2(np.random.permutation(np.resize(levels, k // 32))).repeat(32)
    a = np.empty((k // 512, 16))
    for p in range(k // 512):
        a[p, :8] = np.random.permutation(np.resize(levels, 8))
        for g in range(8):
            far = levels[np.abs(levels - a[p, g]) >= 10]
            a[p, g + 8] = far[np.random.randint(len(far))]
    return np.exp2(a.ravel()).repeat(32)


def f64(x):
    return np.asarray(x).astype(np.float64)


def striped(idx):
    return np.tile(idx.reshape(-1, 16).T, (8, 1)).astype(np.uint16)


def unstriped(offs):
    return offs[:16].T.reshape(-1).astype(np.int64)


E2M1 = np.array([0.0, 0.5, 1.0, 1.5, 2.0, 3.0, 4.0, 6.0, -0.0, -0.5, -1.0, -1.5, -2.0, -3.0, -4.0, -6.0])


def pack_weight(w, fmt):
    k, n = w.shape
    w = f64(np.asarray(w, np.float32).astype(ml_dtypes.bfloat16)).reshape(k // 32, 32, n)
    amax = np.abs(w).max(1)
    if fmt == "e4m3":
        byte = np.frexp(amax)[1] - 1 + 127 - 7
    else:
        mant, ex = np.frexp(amax / 6.0)
        byte = np.where(mant > 0.5, ex, ex - 1) + 127
    byte = np.clip(np.where(amax > 0, byte, 1), 1, 254)
    scaled = (w * np.exp2(127.0 - byte)[:, None, :]).reshape(k, n).astype(np.float32)
    by_word = np.ascontiguousarray(scaled.reshape(k // 512, 128, 4, n).transpose(0, 1, 3, 2))
    if fmt == "e4m3":
        words = by_word.astype(ml_dtypes.float8_e4m3fn).view(np.uint8)
    else:
        c = by_word.astype(ml_dtypes.float4_e2m1fn).view(np.uint8) & 0xF
        words = (c[..., 0::2] | (c[..., 1::2] << 4)).reshape(k // 512, 128, 2 * n)
    return np.ascontiguousarray(words), np.ascontiguousarray(byte.astype(np.uint8).reshape(k // 512, 16, n))


def unpack_weight(words, scales, fmt):
    g, _, n = scales.shape
    words = np.ascontiguousarray(words).reshape(g, 128, n, -1)
    if fmt == "e4m3":
        vals = words.view(ml_dtypes.float8_e4m3fn).astype(np.float64)
    else:
        nib = np.empty((g, 128, n, 4), np.uint8)
        nib[..., 0::2] = words & 0xF
        nib[..., 1::2] = words >> 4
        vals = E2M1[nib]
    vals = vals * np.repeat(np.exp2(scales.astype(np.float64) - 127.0), 8, axis=1)[..., None]
    return vals.transpose(0, 1, 3, 2).reshape(g * 512, n)


def gelu(v):
    return 0.5 * v * (1.0 + np.tanh(np.sqrt(2.0 / np.pi) * (v + 0.044715 * v**3)))


def striped8(idx):
    return np.concatenate([v.reshape(-1, 16).T for v in idx]).astype(np.uint16)


def unstriped8(offs):
    return np.stack([offs[16 * g:16 * g + 16].T.reshape(-1) for g in range(8)]).astype(np.int64)


def runs(v, idx8):
    k = np.arange(v.shape[0])
    return v[k[:, None], idx8[k % 512 // 64]]


def put_heads(h, wgs, idx8, t2):
    r = np.arange(h.shape[0])
    page = np.zeros((h.shape[0], t2))
    page[r[:, None], idx8[r % 512 // 64]] = wgs[r // 4 % 128] * h
    return page


K, H, T, S, T2 = 1024, 1024, 2048, 512, 1024

def setup_inputs():
    n = np.random.standard_normal
    s = mx_kscale(K)[:, None]
    u = mx_kscale(H)[:, None]
    tab_words, tab_scales = pack_weight(n((K, T)) * s, "e4m3")
    offs = striped8(np.stack([np.random.permutation(T)[:S] for _ in range(8)]))
    offs2 = striped8(np.stack([np.random.permutation(T2)[:S] for _ in range(8)]))
    wa = (0.8 * n((K, H)) / np.sqrt(K) / s).astype(np.float32)
    wb_words, wb_scales = pack_weight(0.8 * n((K, H)) / np.sqrt(K) / s, "e2m1")
    sens = (np.random.uniform(0.5, 1.5, H) * u[:, 0]).astype(np.float32)
    wc_words, wc_scales = pack_weight(0.8 * n((H, H)) / np.sqrt(H) / u, "e4m3")
    wgo = np.repeat(np.random.uniform(0.5, 2.0, (8, S)), 16, axis=0).astype(np.float32)
    return {"tab_words": tab_words, "tab_scales": tab_scales, "offs": offs, "wa": wa,
            "wb_words": wb_words, "wb_scales": wb_scales, "sens": sens,
            "wc_words": wc_words, "wc_scales": wc_scales, "wgo": wgo, "offs2": offs2}

def reference(tab_words, tab_scales, offs, wa, wb_words, wb_scales, sens,
              wc_words, wc_scales, wgo, offs2):
    v = runs(unpack_weight(tab_words, tab_scales, "e4m3"), unstriped8(offs))
    a = mxq(f64(wa), 0, "e4m3").T @ v
    b = unpack_weight(wb_words, wb_scales, "e2m1").T @ v
    h = np.abs(a - b) * f64(sens)[:, None]
    c = unpack_weight(wc_words, wc_scales, "e4m3").T @ mxq(h, 0, "e4m3")
    y = np.tanh(c + a)
    return put_heads(y, f64(wgo), unstriped8(offs2), T2)

@@ -1,0 +1,240 @@
+from contextlib import ExitStack
+
+import concourse.mybir as mybir
+from concourse.masks import make_identity
+
+K, H, T, S, T2 = 1024, 1024, 2048, 512, 1024
+FLOPS = 3 * 2 * K * H * S
+
+F32 = mybir.dt.float32
+BF16 = mybir.dt.bfloat16
+I32 = mybir.dt.int32
+U32 = mybir.dt.uint32
+U16 = mybir.dt.uint16
+U8 = mybir.dt.uint8
+FP8X4 = mybir.dt.float8_e4m3fn_x4
+FP4X4 = mybir.dt.float4_e2m1fn_x4
+ACT = mybir.ActivationFunctionType
+ALU = mybir.AluOpType
+
+P = 128
+PACK = 4
+PASS = P * PACK
+PASSES = K // PASS
+HALVES = H // PASS
+QUARTERS = S // P
+
+
+def tile_list_gamelan_slots_kernel(tc, tab_words, tab_scales, offs, wa, wb_words, wb_scales, sens,
+                                             wc_words, wc_scales, wgo, offs2, out):
+    nc = tc.nc
+    with ExitStack() as ctx:
+        keep = ctx.enter_context(tc.tile_pool(name="keep", bufs=1))
+        ring = ctx.enter_context(tc.tile_pool(name="ring", bufs=2))
+        psum = ctx.enter_context(tc.psum_pool(name="psum", bufs=4))
+
+        def held(shape, dtype, name):
+            return keep.tile(shape, dtype, name=name, align_bytes=64)
+
+        offs_sb = keep.tile([P, S // 16], U16, name="offs_sb")
+        offs2_sb = keep.tile([P, S // 16], U16, name="offs2_sb")
+        sens_sb = held([P, HALVES, PACK], F32, "sens_sb")
+        nc.sync.dma_start(offs_sb[:], offs)
+        nc.sync.dma_start(sens_sb[:], sens.rearrange("(b p t) -> p b t", b=HALVES, t=PACK))
+        nc.sync.dma_start(offs2_sb[:], offs2)
+
+        scale_win = [held([P, T], U8, "scale_win%d" % a) for a in range(PASSES)]
+        v_plane = held([P, PASSES, S], U8, "v_plane")
+        wb_plane = held([P, PASSES, H], U8, "wb_plane")
+        for a in range(PASSES):
+            nc.vector.memset(scale_win[a][:].bitcast(I32), 0)
+            nc.sync.dma_start(scale_win[a][0:P:8, :].bitcast(I32), tab_scales[a].bitcast(I32))
+        nc.vector.memset(v_plane[:].bitcast(I32), 0)
+        wc_plane = held([P, PASSES, H], U8, "wc_plane")
+        nc.vector.memset(wc_plane[:].bitcast(I32), 0)
+
+        def load_plane(queue, plane, scales):
+            for d in range(4):
+                queue.dma_start(plane[32 * d:32 * d + 4].bitcast(I32),
+                                    scales[:, 4 * d:4 * d + 4, :].rearrange("a q c -> q a c").bitcast(I32))
+
+        nc.gpsimd.memset(wb_plane[:].bitcast(I32), 0)
+        load_plane(nc.gpsimd, wb_plane, wb_scales)
+
+        warm = held([P, 1], F32, "warm")
+        nc.vector.memset(warm[:], 0.0)
+        warm2 = held([P, 1], F32, "warm2")
+        nc.scalar.activation(warm2[:], warm[:], ACT.Tanh)
+
+        wa_raw = {}
+
+        def staging(shape, dtype, name, lane):
+            return keep.tile(shape, dtype, name=name, tag="staging%d" % lane, align_bytes=64)
+
+        def load_wa(a, b, row_pieces, column_pieces, lane):
+            raw = staging([P, PACK, PASS], F32, "wa_raw", lane)
+            rows = wa[a * PASS:(a + 1) * PASS, b * PASS:(b + 1) * PASS].rearrange("(p i) c -> p i c", i=PACK)
+            di, dc = PACK // row_pieces, PASS // column_pieces
+            for i in range(0, PACK, di):
+                for c in range(0, PASS, dc):
+                    nc.sync.dma_start(raw[:, i:i + di, c:c + dc], rows[:, i:i + di, c:c + dc])
+            wa_raw[a, b] = raw
+
+        tab_win = [staging([P, T], I32, "tab_win", 1 + a) for a in range(PASSES)]
+
+        def load_tab(a):
+            nc.sync.dma_start(tab_win[a][:], tab_words[a].rearrange("p t i -> p (t i)").bitcast(I32))
+
+        wb_sb = [held([P, 2 * H], U8, "wb_sb%d" % a) for a in range(PASSES)]
+        wc_sb = {}
+
+        def load_wc(b):
+            wc_sb[b] = staging([P, PASSES, PASS], I32, "wc_sb", b)
+            words = wc_words.rearrange("a p c i -> p a (c i)")[:, :, b * PASS * PACK:(b + 1) * PASS * PACK]
+            nc.sync.dma_start(wc_sb[b][:], words.bitcast(I32))
+
+        load_wa(0, 0, PACK, 1, 0)
+        nc.sync.dma_start(wb_sb[0][:].bitcast(I32), wb_words[0].bitcast(I32))
+        load_tab(0)
+        load_tab(1)
+        nc.sync.dma_start(wb_sb[1][:].bitcast(I32), wb_words[1].bitcast(I32))
+
+        v_scale = held([P, PASSES, S], U8, "v_scale")
+        for a in range(PASSES):
+            nc.vector.tensor_copy(v_scale[:, a, :], scale_win[a][:].indirect(offs_sb[:]))
+        for r in range(4):
+            nc.sync.dma_start(v_plane[r:P:32].rearrange("p a j -> p (a j)").bitcast(I32),
+                                v_scale[8 * r:P:32].rearrange("p a j -> p (a j)").bitcast(I32))
+        ident = held([P, P], F32, "ident")
+        make_identity(nc, ident[:])
+        load_plane(nc.gpsimd, wc_plane, wc_scales)
+
+        v_codes = [held([P, S], U32, "v_codes%d" % a) for a in range(PASSES)]
+
+        def gather_words(a):
+            nc.vector.tensor_copy(v_codes[a][:], tab_win[a][:].bitcast(U32).indirect(offs_sb[:]))
+
+        wa_codes = {(a, b): held([P, PASS], U32, "wa_codes%d%d" % (a, b)) for a in range(PASSES) for b in range(HALVES)}
+        wa_plane = {(a, b): held([P, PASS], U8, "wa_plane%d%d" % (a, b)) for a in range(PASSES) for b in range(HALVES)}
+
+        def quantize_wa(a, b, column_pieces, copy):
+            grouped = ring.tile([P, PASS, PACK], BF16, name="wa_grouped", tag="grouped", bufs=3, align_bytes=64)
+            dc = PASS // column_pieces
+            for c in range(0, PASS, dc):
+                cols = slice(c, c + dc)
+                copy(grouped[:, cols, :].rearrange("p (c i) t -> p c t i", i=4),
+                     wa_raw[a, b][:, :, cols].rearrange("p t (c i) -> p c t i", i=4))
+                nc.vector.quantize_mx(out=wa_codes[a, b][:, cols].bitcast(FP8X4), scales=wa_plane[a, b][:, cols],
+                                      in_=grouped[:, cols, :].rearrange("p c t -> p (c t)"))
+
+        quantize_wa(0, 0, 1, nc.scalar.copy)
+        load_wa(1, 0, 1, 1, 0)
+        gather_words(0)
+        load_wa(0, 1, 1, 1, 1)
+        gather_words(1)
+        load_wa(1, 1, 1, 2, 2)
+        quantize_wa(1, 0, 1, nc.vector.tensor_copy)
+        load_wc(0)
+        quantize_wa(0, 1, 1, nc.vector.tensor_copy)
+        wgo_sb = ring.tile([P, S], F32, name="wgo_sb", tag="grouped", bufs=3, align_bytes=64)
+        nc.sync.dma_start(wgo_sb[:], wgo)
+        load_wc(1)
+        quantize_wa(1, 1, 2, nc.vector.tensor_copy)
+
+        def entries(q):
+            return slice(q * P, (q + 1) * P)
+
+        def product(stationary, moving):
+            bank = psum.tile([P, PASS], F32, name="mx_bank", tag="mx")
+            for a in range(PASSES):
+                lhs, lhs_scale = stationary(a)
+                rhs, rhs_scale = moving(a)
+                nc.tensor.matmul_mx(out=bank[:], lhsT=lhs, lhsT_scale=lhs_scale, rhs=rhs, rhs_scale=rhs_scale,
+                                    start=(a == 0), stop=(a == PASSES - 1))
+            return bank[:].rearrange("p (m t) -> p t m", t=PACK)
+
+        def v_side(q):
+            return lambda a: (v_codes[a][:, entries(q)].bitcast(FP8X4), v_plane[:, a, entries(q)])
+
+        def wa_side(b):
+            return lambda a: (wa_codes[a, b][:].bitcast(FP8X4), wa_plane[a, b][:])
+
+        def wb_side(b):
+            return lambda a: (wb_sb[a][:, 2 * PASS * b:2 * PASS * (b + 1)].bitcast(FP4X4),
+                              wb_plane[:, a, PASS * b:PASS * (b + 1)])
+
+        def wc_side(b):
+            return lambda a: (wc_sb[b][:, a, :].bitcast(FP8X4), wc_plane[:, a, PASS * b:PASS * (b + 1)])
+
+        h_codes = {(q, b): held([P, P], U32, "h_codes%d%d" % (q, b)) for q in range(QUARTERS) for b in range(HALVES)}
+        h_plane = {(q, b): held([P, P], U8, "h_plane%d%d" % (q, b)) for q in range(QUARTERS) for b in range(HALVES)}
+
+        def h_side(q):
+            return lambda a: (h_codes[q, a][:].bitcast(FP8X4), h_plane[q, a][:])
+
+        def turned_sum(terms):
+            bank = psum.tile([P, PACK, P], F32, name="turn_bank", tag="turn")
+            for n, term in enumerate(terms):
+                for t in range(PACK):
+                    nc.tensor.matmul(bank[:, t, :], lhsT=term[:, t, :], rhs=ident[:], is_transpose=True,
+                                     start=(n == 0 and t == 0), stop=(n == len(terms) - 1 and t == PACK - 1))
+            return bank
+
+        a_sb = {}
+        neg_b = {}
+
+        def first_reading(q, b):
+            a_sb[q, b] = held([P, PACK, P], F32, "a_sb%d%d" % (q, b))
+            nc.scalar.copy(a_sb[q, b][:], product(v_side(q), wa_side(b)))
+
+        def negated_second_reading(q, b):
+            neg_b[q, b] = held([P, PACK, P], F32, "neg_b%d%d" % (q, b))
+            nc.scalar.activation(neg_b[q, b][:], product(v_side(q), wb_side(b)), ACT.Copy, scale=-1.0)
+
+        def quantize_h(q, b, terms):
+            diff = turned_sum(terms)
+            size = ring.tile([P, P, PACK], F32, name="size", tag="size", align_bytes=64)
+            nc.scalar.activation(size[:], diff[:].rearrange("p t j -> p j t"), ACT.Abs)
+            h = ring.tile([P, P, PACK], BF16, name="h", tag="h", align_bytes=64)
+            nc.vector.tensor_tensor(h[:], size[:], sens_sb[:, b:b + 1, :].to_broadcast([P, P, PACK]), ALU.mult)
+            nc.vector.quantize_mx(out=h_codes[q, b][:].bitcast(FP8X4), scales=h_plane[q, b][:],
+                                  in_=h[:].rearrange("p j t -> p (j t)"))
+
+        pages = [held([P, T2], F32, "page%d" % t) for t in range(PACK)]
+        y_sb = {}
+
+        def half_of_h(q, b):
+            negated_second_reading(q, b)
+            first_reading(q, b)
+            quantize_h(q, b, [neg_b[q, b], a_sb[q, b]])
+
+        def cleaned(chunk, b):
+            y_sb[chunk, b] = held([P, PACK, P * len(chunk)], F32, "y_sb%d%d" % (chunk[0], b))
+            for place, q in enumerate(chunk):
+                c_sb = ring.tile([P, PACK, P], F32, name="c_sb", tag="c_sb", align_bytes=64)
+                nc.scalar.copy(c_sb[:], product(h_side(q), wc_side(b)))
+                total = turned_sum([a_sb[q, b], c_sb])
+                nc.scalar.activation(y_sb[chunk, b][:, :, entries(place)], total[:], ACT.Tanh)
+
+        def scatter(chunk, b):
+            lo, hi = chunk[0] * P, (chunk[-1] + 1) * P
+            for t in range(PACK):
+                nc.vector.tensor_tensor(pages[t][:].indirect(offs2_sb[:, lo // 16:hi // 16]),
+                                        y_sb[chunk, b][:, t, :], wgo_sb[:, lo:hi], ALU.mult)
+                if hi == S:
+                    rows = out[b * PASS:(b + 1) * PASS, :].rearrange("(p t) s -> p t s", t=PACK)
+                    nc.sync.dma_start(rows[:, t, :], pages[t][:])
+
+        for q in range(QUARTERS):
+            for b in range(HALVES):
+                half_of_h(q, b)
+            if q > 0:
+                cleaned((q - 1,), 0)
+        cleaned((QUARTERS - 1,), 0)
+        for page in pages:
+            nc.vector.memset(page[:].bitcast(I32), 0)
+        for q in range(QUARTERS):
+            scatter((q,), 0)
+        for chunk in ((0, 1), (2, 3)):
+            cleaned(chunk, 1)
+            scatter(chunk, 1)

@@ -23,6 +23,12 @@ PASS = P * PACK
 PASSES = K // PASS
 HALVES = H // PASS
 QUARTERS = S // P
+QUADRANT = 32
+BLOCK_PARTITIONS = 8
+GROUP = 16
+LINE = 4
+BANKS = 4
+DEPTH = 3
 
 
 def tile_list_gamelan_slots_kernel(tc, tab_words, tab_scales, offs, wa, wb_words, wb_scales, sens,
@@ -30,211 +36,197 @@ def tile_list_gamelan_slots_kernel(tc, tab_words, tab_scales, offs, wa, wb_words
     nc = tc.nc
     with ExitStack() as ctx:
         keep = ctx.enter_context(tc.tile_pool(name="keep", bufs=1))
-        ring = ctx.enter_context(tc.tile_pool(name="ring", bufs=2))
-        psum = ctx.enter_context(tc.psum_pool(name="psum", bufs=4))
+        ring = ctx.enter_context(tc.tile_pool(name="ring", bufs=DEPTH))
+        psum = ctx.enter_context(tc.psum_pool(name="psum", bufs=BANKS))
 
         def held(shape, dtype, name):
             return keep.tile(shape, dtype, name=name, align_bytes=64)
 
-        offs_sb = keep.tile([P, S // 16], U16, name="offs_sb")
-        offs2_sb = keep.tile([P, S // 16], U16, name="offs2_sb")
-        sens_sb = held([P, HALVES, PACK], F32, "sens_sb")
+        def passing(shape, dtype, name):
+            return ring.tile(shape, dtype, name=name, align_bytes=64)
+
+        offs_sb = keep.tile([P, S // GROUP], U16, name="offs_sb")
+        offs2_sb = keep.tile([P, S // GROUP], U16, name="offs2_sb")
         nc.sync.dma_start(offs_sb[:], offs)
-        nc.sync.dma_start(sens_sb[:], sens.rearrange("(b p t) -> p b t", b=HALVES, t=PACK))
-        nc.sync.dma_start(offs2_sb[:], offs2)
-
-        scale_win = [held([P, T], U8, "scale_win%d" % a) for a in range(PASSES)]
-        v_plane = held([P, PASSES, S], U8, "v_plane")
-        wb_plane = held([P, PASSES, H], U8, "wb_plane")
-        for a in range(PASSES):
-            nc.vector.memset(scale_win[a][:].bitcast(I32), 0)
-            nc.sync.dma_start(scale_win[a][0:P:8, :].bitcast(I32), tab_scales[a].bitcast(I32))
-        nc.vector.memset(v_plane[:].bitcast(I32), 0)
-        wc_plane = held([P, PASSES, H], U8, "wc_plane")
-        nc.vector.memset(wc_plane[:].bitcast(I32), 0)
-
-        def load_plane(queue, plane, scales):
-            for d in range(4):
-                queue.dma_start(plane[32 * d:32 * d + 4].bitcast(I32),
-                                    scales[:, 4 * d:4 * d + 4, :].rearrange("a q c -> q a c").bitcast(I32))
-
-        nc.gpsimd.memset(wb_plane[:].bitcast(I32), 0)
-        load_plane(nc.gpsimd, wb_plane, wb_scales)
-
-        warm = held([P, 1], F32, "warm")
-        nc.vector.memset(warm[:], 0.0)
-        warm2 = held([P, 1], F32, "warm2")
-        nc.scalar.activation(warm2[:], warm[:], ACT.Tanh)
 
         wa_raw = {}
 
-        def staging(shape, dtype, name, lane):
-            return keep.tile(shape, dtype, name=name, tag="staging%d" % lane, align_bytes=64)
+        def load_wa(g, half):
+            wa_raw[g, half] = held([P, PACK, PASS], F32, "wa_raw%d%d" % (g, half))
+            rows = wa[g * PASS:(g + 1) * PASS, half * PASS:(half + 1) * PASS]
+            nc.sync.dma_start(wa_raw[g, half][:], rows.rearrange("(p i) c -> p i c", i=PACK))
 
-        def load_wa(a, b, row_pieces, column_pieces, lane):
-            raw = staging([P, PACK, PASS], F32, "wa_raw", lane)
-            rows = wa[a * PASS:(a + 1) * PASS, b * PASS:(b + 1) * PASS].rearrange("(p i) c -> p i c", i=PACK)
-            di, dc = PACK // row_pieces, PASS // column_pieces
-            for i in range(0, PACK, di):
-                for c in range(0, PASS, dc):
-                    nc.sync.dma_start(raw[:, i:i + di, c:c + dc], rows[:, i:i + di, c:c + dc])
-            wa_raw[a, b] = raw
+        load_wa(0, 0)
 
-        tab_win = [staging([P, T], I32, "tab_win", 1 + a) for a in range(PASSES)]
+        scale_window = [held([P, T], U8, "scale_window%d" % g) for g in range(PASSES)]
+        for g in range(PASSES):
+            nc.vector.memset(scale_window[g][:].bitcast(I32), 0)
+            nc.sync.dma_start(scale_window[g][0:P:BLOCK_PARTITIONS, :].bitcast(I32), tab_scales[g].bitcast(I32))
 
-        def load_tab(a):
-            nc.sync.dma_start(tab_win[a][:], tab_words[a].rearrange("p t i -> p (t i)").bitcast(I32))
+        v_plane = held([P, PASSES, S], U8, "v_plane")
+        wb_plane = held([P, PASSES, H], U8, "wb_plane")
+        wc_plane = held([P, PASSES, H], U8, "wc_plane")
+        nc.vector.memset(v_plane[:].bitcast(I32), 0)
+        nc.vector.memset(wc_plane[:].bitcast(I32), 0)
+        nc.gpsimd.memset(wb_plane[:].bitcast(I32), 0)
 
-        wb_sb = [held([P, 2 * H], U8, "wb_sb%d" % a) for a in range(PASSES)]
-        wc_sb = {}
+        def load_plane(plane, scales):
+            for d in range(P // QUADRANT):
+                nc.gpsimd.dma_start(plane[QUADRANT * d:QUADRANT * d + 4].bitcast(I32),
+                                    scales[:, 4 * d:4 * d + 4, :].rearrange("g q c -> q g c").bitcast(I32))
 
-        def load_wc(b):
-            wc_sb[b] = staging([P, PASSES, PASS], I32, "wc_sb", b)
-            words = wc_words.rearrange("a p c i -> p a (c i)")[:, :, b * PASS * PACK:(b + 1) * PASS * PACK]
-            nc.sync.dma_start(wc_sb[b][:], words.bitcast(I32))
+        load_plane(wb_plane, wb_scales)
 
-        load_wa(0, 0, PACK, 1, 0)
-        nc.sync.dma_start(wb_sb[0][:].bitcast(I32), wb_words[0].bitcast(I32))
-        load_tab(0)
-        load_tab(1)
-        nc.sync.dma_start(wb_sb[1][:].bitcast(I32), wb_words[1].bitcast(I32))
+        sens_sb = held([P, HALVES, PACK], F32, "sens_sb")
+        nc.scalar.dma_start(sens_sb[:], sens.rearrange("(half m t) -> m half t", half=HALVES, t=PACK))
+
+        word_window = [held([P, T], I32, "word_window%d" % g) for g in range(PASSES)]
+        for g in range(PASSES):
+            nc.sync.dma_start(word_window[g][:], tab_words[g].rearrange("p t i -> p (t i)").bitcast(I32))
+        wb_sb = held([P, PASSES, 2 * H], U8, "wb_sb")
+        nc.sync.dma_start(wb_sb[:].bitcast(I32), wb_words.rearrange("g p c -> p g c").bitcast(I32))
 
         v_scale = held([P, PASSES, S], U8, "v_scale")
-        for a in range(PASSES):
-            nc.vector.tensor_copy(v_scale[:, a, :], scale_win[a][:].indirect(offs_sb[:]))
+        for g in range(PASSES):
+            nc.vector.tensor_copy(v_scale[:, g, :], scale_window[g][:].indirect(offs_sb[:]))
         for r in range(4):
-            nc.sync.dma_start(v_plane[r:P:32].rearrange("p a j -> p (a j)").bitcast(I32),
-                                v_scale[8 * r:P:32].rearrange("p a j -> p (a j)").bitcast(I32))
+            nc.sync.dma_start(v_plane[r:P:QUADRANT].rearrange("p g j -> p (g j)").bitcast(I32),
+                              v_scale[BLOCK_PARTITIONS * r:P:QUADRANT].rearrange("p g j -> p (g j)").bitcast(I32))
+
+        wc_sb = [held([P, PASSES, PASS], I32, "wc_sb%d" % half) for half in range(HALVES)]
+
+        def load_wc(half):
+            words = wc_words.rearrange("g p c i -> p g (c i)")[:, :, half * PASS * PACK:(half + 1) * PASS * PACK]
+            nc.sync.dma_start(wc_sb[half][:], words.bitcast(I32))
+
+        load_wa(1, 0)
+        load_wa(0, 1)
+        load_wa(1, 1)
+        load_wc(0)
+        wgo_sb = held([P, S], F32, "wgo_sb")
+        nc.sync.dma_start(wgo_sb[:], wgo)
+        nc.sync.dma_start(offs2_sb[:], offs2)
+        load_wc(1)
+
         ident = held([P, P], F32, "ident")
         make_identity(nc, ident[:])
-        load_plane(nc.gpsimd, wc_plane, wc_scales)
+        load_plane(wc_plane, wc_scales)
 
-        v_codes = [held([P, S], U32, "v_codes%d" % a) for a in range(PASSES)]
+        v_codes = [held([P, S], U32, "v_codes%d" % g) for g in range(PASSES)]
+        for g in range(PASSES):
+            nc.vector.tensor_copy(v_codes[g][:], word_window[g][:].bitcast(U32).indirect(offs_sb[:]))
 
-        def gather_words(a):
-            nc.vector.tensor_copy(v_codes[a][:], tab_win[a][:].bitcast(U32).indirect(offs_sb[:]))
+        wa_codes, wa_plane = {}, {}
+        for half in range(HALVES):
+            for g in range(PASSES):
+                grouped = held([P, PASS, PACK], BF16, "wa_grouped%d%d" % (g, half))
+                to = grouped[:].rearrange("p (c e) i -> p c i e", e=LINE)
+                source = wa_raw[g, half][:].rearrange("p i (c e) -> p c i e", e=LINE)
+                if (g, half) == (0, 0):
+                    nc.scalar.activation(to, source, ACT.Copy)
+                else:
+                    nc.vector.tensor_copy(to, source)
+                wa_codes[g, half] = held([P, PASS], U32, "wa_codes%d%d" % (g, half))
+                wa_plane[g, half] = held([P, PASS], U8, "wa_plane%d%d" % (g, half))
+                nc.vector.quantize_mx(out=wa_codes[g, half][:].bitcast(FP8X4), scales=wa_plane[g, half][:],
+                                      in_=grouped[:].rearrange("p c i -> p (c i)"))
 
-        wa_codes = {(a, b): held([P, PASS], U32, "wa_codes%d%d" % (a, b)) for a in range(PASSES) for b in range(HALVES)}
-        wa_plane = {(a, b): held([P, PASS], U8, "wa_plane%d%d" % (a, b)) for a in range(PASSES) for b in range(HALVES)}
-
-        def quantize_wa(a, b, column_pieces, copy):
-            grouped = ring.tile([P, PASS, PACK], BF16, name="wa_grouped", tag="grouped", bufs=3, align_bytes=64)
-            dc = PASS // column_pieces
-            for c in range(0, PASS, dc):
-                cols = slice(c, c + dc)
-                copy(grouped[:, cols, :].rearrange("p (c i) t -> p c t i", i=4),
-                     wa_raw[a, b][:, :, cols].rearrange("p t (c i) -> p c t i", i=4))
-                nc.vector.quantize_mx(out=wa_codes[a, b][:, cols].bitcast(FP8X4), scales=wa_plane[a, b][:, cols],
-                                      in_=grouped[:, cols, :].rearrange("p c t -> p (c t)"))
-
-        quantize_wa(0, 0, 1, nc.scalar.copy)
-        load_wa(1, 0, 1, 1, 0)
-        gather_words(0)
-        load_wa(0, 1, 1, 1, 1)
-        gather_words(1)
-        load_wa(1, 1, 1, 2, 2)
-        quantize_wa(1, 0, 1, nc.vector.tensor_copy)
-        load_wc(0)
-        quantize_wa(0, 1, 1, nc.vector.tensor_copy)
-        wgo_sb = ring.tile([P, S], F32, name="wgo_sb", tag="grouped", bufs=3, align_bytes=64)
-        nc.sync.dma_start(wgo_sb[:], wgo)
-        load_wc(1)
-        quantize_wa(1, 1, 2, nc.vector.tensor_copy)
+        h_codes, h_plane = {}, {}
 
         def entries(q):
             return slice(q * P, (q + 1) * P)
 
+        def channels(half):
+            return slice(half * PASS, (half + 1) * PASS)
+
+        def v_operand(q):
+            return lambda g: (v_codes[g][:, entries(q)].bitcast(FP8X4), v_plane[:, g, entries(q)])
+
+        def h_operand(q):
+            return lambda g: (h_codes[q, g][:].bitcast(FP8X4), h_plane[q, g][:])
+
+        def wa_operand(half):
+            return lambda g: (wa_codes[g, half][:].bitcast(FP8X4), wa_plane[g, half][:])
+
+        def wb_operand(half):
+            return lambda g: (wb_sb[:, g, 2 * PASS * half:2 * PASS * (half + 1)].bitcast(FP4X4),
+                              wb_plane[:, g, channels(half)])
+
+        def wc_operand(half):
+            return lambda g: (wc_sb[half][:, g, :].bitcast(FP8X4), wc_plane[:, g, channels(half)])
+
         def product(stationary, moving):
-            bank = psum.tile([P, PASS], F32, name="mx_bank", tag="mx")
-            for a in range(PASSES):
-                lhs, lhs_scale = stationary(a)
-                rhs, rhs_scale = moving(a)
+            bank = psum.tile([P, PASS], F32, name="product_bank")
+            for g in range(PASSES):
+                (lhs, lhs_scale), (rhs, rhs_scale) = stationary(g), moving(g)
                 nc.tensor.matmul_mx(out=bank[:], lhsT=lhs, lhsT_scale=lhs_scale, rhs=rhs, rhs_scale=rhs_scale,
-                                    start=(a == 0), stop=(a == PASSES - 1))
+                                    start=(g == 0), stop=(g == PASSES - 1))
             return bank[:].rearrange("p (m t) -> p t m", t=PACK)
 
-        def v_side(q):
-            return lambda a: (v_codes[a][:, entries(q)].bitcast(FP8X4), v_plane[:, a, entries(q)])
-
-        def wa_side(b):
-            return lambda a: (wa_codes[a, b][:].bitcast(FP8X4), wa_plane[a, b][:])
-
-        def wb_side(b):
-            return lambda a: (wb_sb[a][:, 2 * PASS * b:2 * PASS * (b + 1)].bitcast(FP4X4),
-                              wb_plane[:, a, PASS * b:PASS * (b + 1)])
-
-        def wc_side(b):
-            return lambda a: (wc_sb[b][:, a, :].bitcast(FP8X4), wc_plane[:, a, PASS * b:PASS * (b + 1)])
-
-        h_codes = {(q, b): held([P, P], U32, "h_codes%d%d" % (q, b)) for q in range(QUARTERS) for b in range(HALVES)}
-        h_plane = {(q, b): held([P, P], U8, "h_plane%d%d" % (q, b)) for q in range(QUARTERS) for b in range(HALVES)}
-
-        def h_side(q):
-            return lambda a: (h_codes[q, a][:].bitcast(FP8X4), h_plane[q, a][:])
-
-        def turned_sum(terms):
-            bank = psum.tile([P, PACK, P], F32, name="turn_bank", tag="turn")
-            for n, term in enumerate(terms):
+        def transposed_sum(first, second):
+            bank = psum.tile([P, PACK, P], F32, name="sum_bank")
+            for term in (first, second):
                 for t in range(PACK):
                     nc.tensor.matmul(bank[:, t, :], lhsT=term[:, t, :], rhs=ident[:], is_transpose=True,
-                                     start=(n == 0 and t == 0), stop=(n == len(terms) - 1 and t == PACK - 1))
+                                     start=(term is first and t == 0), stop=(term is second and t == PACK - 1))
             return bank
 
-        a_sb = {}
-        neg_b = {}
+        a_sb, minus_b = {}, {}
 
-        def first_reading(q, b):
-            a_sb[q, b] = held([P, PACK, P], F32, "a_sb%d%d" % (q, b))
-            nc.scalar.copy(a_sb[q, b][:], product(v_side(q), wa_side(b)))
+        def make_minus_b(q, half):
+            minus_b[q, half] = held([P, PACK, P], F32, "minus_b%d%d" % (q, half))
+            nc.scalar.activation(minus_b[q, half][:], product(v_operand(q), wb_operand(half)), ACT.Copy, scale=-1.0)
 
-        def negated_second_reading(q, b):
-            neg_b[q, b] = held([P, PACK, P], F32, "neg_b%d%d" % (q, b))
-            nc.scalar.activation(neg_b[q, b][:], product(v_side(q), wb_side(b)), ACT.Copy, scale=-1.0)
+        def make_h(q, half):
+            a_sb[q, half] = held([P, PACK, P], F32, "a_sb%d%d" % (q, half))
+            nc.scalar.copy(a_sb[q, half][:], product(v_operand(q), wa_operand(half)))
+            difference = transposed_sum(minus_b[q, half], a_sb[q, half])
+            size = passing([P, P, PACK], F32, "size")
+            nc.scalar.activation(size[:], difference[:].rearrange("m t j -> m j t"), ACT.Abs)
+            h = passing([P, P, PACK], BF16, "h")
+            nc.vector.tensor_tensor(h[:], size[:], sens_sb[:, half:half + 1, :].to_broadcast([P, P, PACK]), ALU.mult)
+            h_codes[q, half] = held([P, P], U32, "h_codes%d%d" % (q, half))
+            h_plane[q, half] = held([P, P], U8, "h_plane%d%d" % (q, half))
+            nc.vector.quantize_mx(out=h_codes[q, half][:].bitcast(FP8X4), scales=h_plane[q, half][:],
+                                  in_=h[:].rearrange("m j t -> m (j t)"))
 
-        def quantize_h(q, b, terms):
-            diff = turned_sum(terms)
-            size = ring.tile([P, P, PACK], F32, name="size", tag="size", align_bytes=64)
-            nc.scalar.activation(size[:], diff[:].rearrange("p t j -> p j t"), ACT.Abs)
-            h = ring.tile([P, P, PACK], BF16, name="h", tag="h", align_bytes=64)
-            nc.vector.tensor_tensor(h[:], size[:], sens_sb[:, b:b + 1, :].to_broadcast([P, P, PACK]), ALU.mult)
-            nc.vector.quantize_mx(out=h_codes[q, b][:].bitcast(FP8X4), scales=h_plane[q, b][:],
-                                  in_=h[:].rearrange("p j t -> p (j t)"))
-
-        pages = [held([P, T2], F32, "page%d" % t) for t in range(PACK)]
         y_sb = {}
 
-        def half_of_h(q, b):
-            negated_second_reading(q, b)
-            first_reading(q, b)
-            quantize_h(q, b, [neg_b[q, b], a_sb[q, b]])
+        def make_y(quarters, half):
+            y_sb[quarters, half] = held([P, PACK, P * len(quarters)], F32, "y_sb%d%d" % (quarters[0], half))
+            for place, q in enumerate(quarters):
+                c_sb = passing([P, PACK, P], F32, "c_sb")
+                nc.scalar.copy(c_sb[:], product(h_operand(q), wc_operand(half)))
+                total = transposed_sum(a_sb[q, half], c_sb)
+                nc.scalar.activation(y_sb[quarters, half][:, :, entries(place)], total[:], ACT.Tanh)
 
-        def cleaned(chunk, b):
-            y_sb[chunk, b] = held([P, PACK, P * len(chunk)], F32, "y_sb%d%d" % (chunk[0], b))
-            for place, q in enumerate(chunk):
-                c_sb = ring.tile([P, PACK, P], F32, name="c_sb", tag="c_sb", align_bytes=64)
-                nc.scalar.copy(c_sb[:], product(h_side(q), wc_side(b)))
-                total = turned_sum([a_sb[q, b], c_sb])
-                nc.scalar.activation(y_sb[chunk, b][:, :, entries(place)], total[:], ACT.Tanh)
+        pages = [held([P, T2], F32, "page%d" % t) for t in range(PACK)]
 
-        def scatter(chunk, b):
-            lo, hi = chunk[0] * P, (chunk[-1] + 1) * P
+        def scatter(quarters, half):
+            lo, hi = quarters[0] * P, (quarters[-1] + 1) * P
+            rows = out[channels(half), :].rearrange("(m t) s -> m t s", t=PACK)
             for t in range(PACK):
-                nc.vector.tensor_tensor(pages[t][:].indirect(offs2_sb[:, lo // 16:hi // 16]),
-                                        y_sb[chunk, b][:, t, :], wgo_sb[:, lo:hi], ALU.mult)
+                nc.vector.tensor_tensor(pages[t][:].indirect(offs2_sb[:, lo // GROUP:hi // GROUP]),
+                                        y_sb[quarters, half][:, t, :], wgo_sb[:, lo:hi], ALU.mult)
                 if hi == S:
-                    rows = out[b * PASS:(b + 1) * PASS, :].rearrange("(p t) s -> p t s", t=PACK)
                     nc.sync.dma_start(rows[:, t, :], pages[t][:])
 
+        for half in range(HALVES):
+            for q in range(QUARTERS):
+                make_minus_b(q, half)
         for q in range(QUARTERS):
-            for b in range(HALVES):
-                half_of_h(q, b)
-            if q > 0:
-                cleaned((q - 1,), 0)
-        cleaned((QUARTERS - 1,), 0)
+            make_h(q, 0)
+        for q in range(QUARTERS - 1):
+            make_h(q, 1)
+        runs = [(0,), (1,), (2, 3)]
+        make_y(runs[0], 0)
+        make_h(QUARTERS - 1, 1)
+        for run in runs[1:]:
+            make_y(run, 0)
         for page in pages:
             nc.vector.memset(page[:].bitcast(I32), 0)
-        for q in range(QUARTERS):
-            scatter((q,), 0)
-        for chunk in ((0, 1), (2, 3)):
-            cleaned(chunk, 1)
-            scatter(chunk, 1)
+        for run in runs:
+            scatter(run, 0)
+        whole = tuple(range(QUARTERS))
+        make_y(whole, 1)
+        scatter(whole, 1)

@@ -161,7 +161,10 @@ def tile_list_gamelan_slots_kernel(tc, tab_words, tab_scales, offs, wa, wb_words
                 (lhs, lhs_scale), (rhs, rhs_scale) = stationary(g), moving(g)
                 nc.tensor.matmul_mx(out=bank[:], lhsT=lhs, lhsT_scale=lhs_scale, rhs=rhs, rhs_scale=rhs_scale,
                                     start=(g == 0), stop=(g == PASSES - 1))
-            return bank[:].rearrange("p (m t) -> p t m", t=PACK)
+            return bank[:].rearrange("p (m u e) -> p u m e", u=2, e=2)
+
+        def by_pairs(tile):
+            return tile[:].rearrange("p (u e) m -> p u m e", e=2)
 
         def transposed_sum(first, second):
             bank = psum.tile([P, PACK, P], F32, name="sum_bank")
@@ -175,11 +178,11 @@ def tile_list_gamelan_slots_kernel(tc, tab_words, tab_scales, offs, wa, wb_words
 
         def make_minus_b(q, half):
             minus_b[q, half] = held([P, PACK, P], F32, "minus_b%d%d" % (q, half))
-            nc.scalar.activation(minus_b[q, half][:], product(v_operand(q), wb_operand(half)), ACT.Copy, scale=-1.0)
+            nc.scalar.activation(by_pairs(minus_b[q, half]), product(v_operand(q), wb_operand(half)), ACT.Copy, scale=-1.0)
 
         def make_h(q, half):
             a_sb[q, half] = held([P, PACK, P], F32, "a_sb%d%d" % (q, half))
-            nc.scalar.copy(a_sb[q, half][:], product(v_operand(q), wa_operand(half)))
+            nc.scalar.copy(by_pairs(a_sb[q, half]), product(v_operand(q), wa_operand(half)))
             difference = transposed_sum(minus_b[q, half], a_sb[q, half])
             size = passing([P, P, PACK], F32, "size")
             nc.scalar.activation(size[:], difference[:].rearrange("m t j -> m j t"), ACT.Abs)
@@ -196,7 +199,7 @@ def tile_list_gamelan_slots_kernel(tc, tab_words, tab_scales, offs, wa, wb_words
             y_sb[quarters, half] = held([P, PACK, P * len(quarters)], F32, "y_sb%d%d" % (quarters[0], half))
             for place, q in enumerate(quarters):
                 c_sb = passing([P, PACK, P], F32, "c_sb")
-                nc.scalar.copy(c_sb[:], product(h_operand(q), wc_operand(half)))
+                nc.scalar.copy(by_pairs(c_sb), product(h_operand(q), wc_operand(half)))
                 total = transposed_sum(a_sb[q, half], c_sb)
                 nc.scalar.activation(y_sb[quarters, half][:, :, entries(place)], total[:], ACT.Tanh)
 

@@ -28,6 +28,7 @@ BLOCK_PARTITIONS = 8
 GROUP = 16
 LINE = 4
 BANKS = 4
+PIECE = 256
 DEPTH = 3
 
 
@@ -37,7 +38,8 @@ def tile_list_gamelan_slots_kernel(tc, tab_words, tab_scales, offs, wa, wb_words
     with ExitStack() as ctx:
         keep = ctx.enter_context(tc.tile_pool(name="keep", bufs=1))
         ring = ctx.enter_context(tc.tile_pool(name="ring", bufs=DEPTH))
-        psum = ctx.enter_context(tc.psum_pool(name="psum", bufs=BANKS))
+        shared = ctx.enter_context(tc.tile_pool(name="shared", bufs=1))
+        psum = ctx.enter_context(tc.psum_pool(name="psum", bufs=1))
 
         def held(shape, dtype, name):
             return keep.tile(shape, dtype, name=name, align_bytes=64)
@@ -45,18 +47,14 @@ def tile_list_gamelan_slots_kernel(tc, tab_words, tab_scales, offs, wa, wb_words
         def passing(shape, dtype, name):
             return ring.tile(shape, dtype, name=name, align_bytes=64)
 
+        def placed(shape, dtype, name, kib):
+            return shared.tile(shape, dtype, name=name, align_bytes=64, offset=kib * 1024)
+
         offs_sb = keep.tile([P, S // GROUP], U16, name="offs_sb")
         offs2_sb = keep.tile([P, S // GROUP], U16, name="offs2_sb")
         nc.sync.dma_start(offs_sb[:], offs)
-
-        wa_raw = {}
-
-        def load_wa(g, half):
-            wa_raw[g, half] = held([P, PACK, PASS], F32, "wa_raw%d%d" % (g, half))
-            rows = wa[g * PASS:(g + 1) * PASS, half * PASS:(half + 1) * PASS]
-            nc.sync.dma_start(wa_raw[g, half][:], rows.rearrange("(p i) c -> p i c", i=PACK))
-
-        load_wa(0, 0)
+        wb_sb = held([P, PASSES, 2 * H], U8, "wb_sb")
+        nc.sync.dma_start(wb_sb[:].bitcast(I32), wb_words.rearrange("g p c -> p g c").bitcast(I32))
 
         scale_window = [held([P, T], U8, "scale_window%d" % g) for g in range(PASSES)]
         for g in range(PASSES):
@@ -65,26 +63,24 @@ def tile_list_gamelan_slots_kernel(tc, tab_words, tab_scales, offs, wa, wb_words
 
         v_plane = held([P, PASSES, S], U8, "v_plane")
         wb_plane = held([P, PASSES, H], U8, "wb_plane")
-        wc_plane = held([P, PASSES, H], U8, "wc_plane")
         nc.vector.memset(v_plane[:].bitcast(I32), 0)
-        nc.vector.memset(wc_plane[:].bitcast(I32), 0)
         nc.gpsimd.memset(wb_plane[:].bitcast(I32), 0)
 
-        def load_plane(plane, scales):
-            for d in range(P // QUADRANT):
-                nc.gpsimd.dma_start(plane[QUADRANT * d:QUADRANT * d + 4].bitcast(I32),
-                                    scales[:, 4 * d:4 * d + 4, :].rearrange("g q c -> q g c").bitcast(I32))
+        def load_plane(plane, scales, queues):
+            for r, queue in enumerate(queues):
+                queue.dma_start(plane[r:P:QUADRANT].bitcast(I32),
+                                scales[:, r:16:4, :].rearrange("g d c -> d g c").bitcast(I32))
 
-        load_plane(wb_plane, wb_scales)
+        load_plane(wb_plane, wb_scales, [nc.sync] * 4)
 
+        ident = held([P, P], F32, "ident")
+        make_identity(nc, ident[:])
         sens_sb = held([P, HALVES, PACK], F32, "sens_sb")
-        nc.scalar.dma_start(sens_sb[:], sens.rearrange("(half m t) -> m half t", half=HALVES, t=PACK))
+        nc.gpsimd.dma_start(sens_sb[:], sens.rearrange("(half m t) -> m half t", half=HALVES, t=PACK))
 
         word_window = [held([P, T], I32, "word_window%d" % g) for g in range(PASSES)]
         for g in range(PASSES):
             nc.sync.dma_start(word_window[g][:], tab_words[g].rearrange("p t i -> p (t i)").bitcast(I32))
-        wb_sb = held([P, PASSES, 2 * H], U8, "wb_sb")
-        nc.sync.dma_start(wb_sb[:].bitcast(I32), wb_words.rearrange("g p c -> p g c").bitcast(I32))
 
         v_scale = held([P, PASSES, S], U8, "v_scale")
         for g in range(PASSES):
@@ -93,43 +89,57 @@ def tile_list_gamelan_slots_kernel(tc, tab_words, tab_scales, offs, wa, wb_words
             nc.sync.dma_start(v_plane[r:P:QUADRANT].rearrange("p g j -> p (g j)").bitcast(I32),
                               v_scale[BLOCK_PARTITIONS * r:P:QUADRANT].rearrange("p g j -> p (g j)").bitcast(I32))
 
+        v_codes = [held([P, S], U32, "v_codes%d" % g) for g in range(PASSES)]
+        for g in range(PASSES):
+            width = S if g == 0 else S // 2
+            for lo in range(0, S, width):
+                nc.vector.tensor_copy(v_codes[g][:, lo:lo + width], word_window[g][:].bitcast(U32).indirect(
+                    offs_sb[:, lo // GROUP:(lo + width) // GROUP]))
+
+        wa_pieces = []
+        wa_pieces.append((0, 0, PASS))
+        for half, g in ((0, 1), (1, 0), (1, 1)):
+            for lo in range(0, PASS, PIECE):
+                wa_pieces.append((g, half * PASS + lo, PIECE))
+        wa_raw = {}
+        for g, lo, width in wa_pieces:
+            name = "wa_raw%d_%d" % (g, lo)
+            last = (g, lo, width) == wa_pieces[-1]
+            wa_raw[g, lo] = placed([P, PACK, width], F32, name, 0) if last else held([P, PACK, width], F32, name)
+            rows = wa[g * PASS:(g + 1) * PASS, lo:lo + width]
+            nc.sync.dma_start(wa_raw[g, lo][:], rows.rearrange("(p i) c -> p i c", i=PACK))
+
         wc_sb = [held([P, PASSES, PASS], I32, "wc_sb%d" % half) for half in range(HALVES)]
 
         def load_wc(half):
             words = wc_words.rearrange("g p c i -> p g (c i)")[:, :, half * PASS * PACK:(half + 1) * PASS * PACK]
             nc.sync.dma_start(wc_sb[half][:], words.bitcast(I32))
 
-        load_wa(1, 0)
-        load_wa(0, 1)
-        load_wa(1, 1)
         load_wc(0)
+        wc_plane = held([P, PASSES, H], U8, "wc_plane")
+        nc.gpsimd.memset(wc_plane[:].bitcast(I32), 0)
+        load_plane(wc_plane, wc_scales, [nc.sync] * 4)
+
+        load_wc(1)
         wgo_sb = held([P, S], F32, "wgo_sb")
         nc.sync.dma_start(wgo_sb[:], wgo)
         nc.sync.dma_start(offs2_sb[:], offs2)
-        load_wc(1)
 
-        ident = held([P, P], F32, "ident")
-        make_identity(nc, ident[:])
-        load_plane(wc_plane, wc_scales)
-
-        v_codes = [held([P, S], U32, "v_codes%d" % g) for g in range(PASSES)]
-        for g in range(PASSES):
-            nc.vector.tensor_copy(v_codes[g][:], word_window[g][:].bitcast(U32).indirect(offs_sb[:]))
 
         wa_codes, wa_plane = {}, {}
         for half in range(HALVES):
             for g in range(PASSES):
-                grouped = held([P, PASS, PACK], BF16, "wa_grouped%d%d" % (g, half))
-                to = grouped[:].rearrange("p (c e) i -> p c i e", e=LINE)
-                source = wa_raw[g, half][:].rearrange("p i (c e) -> p c i e", e=LINE)
-                if (g, half) == (0, 0):
-                    nc.scalar.activation(to, source, ACT.Copy)
-                else:
-                    nc.vector.tensor_copy(to, source)
                 wa_codes[g, half] = held([P, PASS], U32, "wa_codes%d%d" % (g, half))
                 wa_plane[g, half] = held([P, PASS], U8, "wa_plane%d%d" % (g, half))
-                nc.vector.quantize_mx(out=wa_codes[g, half][:].bitcast(FP8X4), scales=wa_plane[g, half][:],
-                                      in_=grouped[:].rearrange("p c i -> p (c i)"))
+        for g, lo, width in wa_pieces:
+            grouped = held([P, width, PACK], BF16, "wa_grouped%d_%d" % (g, lo))
+            to = grouped[:].rearrange("p (c e) i -> p c i e", e=LINE)
+            source = wa_raw[g, lo][:].rearrange("p i (c e) -> p c i e", e=LINE)
+            nc.vector.tensor_copy(to, source)
+            half, columns = lo // PASS, slice(lo % PASS, lo % PASS + width)
+            nc.vector.quantize_mx(out=wa_codes[g, half][:, columns].bitcast(FP8X4),
+                                  scales=wa_plane[g, half][:, columns],
+                                  in_=grouped[:].rearrange("p c i -> p (c i)"))
 
         h_codes, h_plane = {}, {}
 
@@ -155,19 +165,20 @@ def tile_list_gamelan_slots_kernel(tc, tab_words, tab_scales, offs, wa, wb_words
         def wc_operand(half):
             return lambda g: (wc_sb[half][:, g, :].bitcast(FP8X4), wc_plane[:, g, channels(half)])
 
-        def product(stationary, moving):
-            bank = psum.tile([P, PASS], F32, name="product_bank")
-            for g in range(PASSES):
+        banks = [psum.tile([P, PASS], F32, name="bank%d" % i) for i in range(2 * BANKS)]
+
+        def product(bank, stationary, moving, order=(0, 1)):
+            for g in order:
                 (lhs, lhs_scale), (rhs, rhs_scale) = stationary(g), moving(g)
                 nc.tensor.matmul_mx(out=bank[:], lhsT=lhs, lhsT_scale=lhs_scale, rhs=rhs, rhs_scale=rhs_scale,
-                                    start=(g == 0), stop=(g == PASSES - 1))
+                                    start=(g == order[0]), stop=(g == order[-1]))
             return bank[:].rearrange("p (m u e) -> p u m e", u=2, e=2)
 
         def by_pairs(tile):
             return tile[:].rearrange("p (u e) m -> p u m e", e=2)
 
-        def transposed_sum(first, second):
-            bank = psum.tile([P, PACK, P], F32, name="sum_bank")
+        def transposed_sum(bank, first, second):
+            bank = bank[:].rearrange("m (t j) -> m t j", t=PACK)
             for term in (first, second):
                 for t in range(PACK):
                     nc.tensor.matmul(bank[:, t, :], lhsT=term[:, t, :], rhs=ident[:], is_transpose=True,
@@ -176,60 +187,127 @@ def tile_list_gamelan_slots_kernel(tc, tab_words, tab_scales, offs, wa, wb_words
 
         a_sb, minus_b = {}, {}
 
-        def make_minus_b(q, half):
+        def make_minus_b(q, half, bank):
             minus_b[q, half] = held([P, PACK, P], F32, "minus_b%d%d" % (q, half))
-            nc.scalar.activation(by_pairs(minus_b[q, half]), product(v_operand(q), wb_operand(half)), ACT.Copy, scale=-1.0)
+            nc.scalar.activation(by_pairs(minus_b[q, half]), product(bank, v_operand(q), wb_operand(half)),
+                                 ACT.Copy, scale=-1.0)
 
-        def make_h(q, half):
+        def make_a(q, half, pb, early):
             a_sb[q, half] = held([P, PACK, P], F32, "a_sb%d%d" % (q, half))
-            nc.scalar.copy(by_pairs(a_sb[q, half]), product(v_operand(q), wa_operand(half)))
-            difference = transposed_sum(minus_b[q, half], a_sb[q, half])
+            nc.scalar.copy(by_pairs(a_sb[q, half]),
+                           product(banks[pb], v_operand(q), wa_operand(half), (0, 1) if early else (1, 0)))
+
+        def make_a_in_pieces(q, half, pbs):
+            a_sb[q, half] = held([P, PACK, P], F32, "a_sb%d%d" % (q, half))
+            for n, pb in enumerate(pbs):
+                columns = slice(n * PIECE, (n + 1) * PIECE)
+                for g in range(PASSES):
+                    lhs, lhs_scale = v_operand(q)(g)
+                    nc.tensor.matmul_mx(out=banks[pb][:, 0:PIECE], lhsT=lhs, lhsT_scale=lhs_scale,
+                                        rhs=wa_codes[g, half][:, columns].bitcast(FP8X4),
+                                        rhs_scale=wa_plane[g, half][:, columns],
+                                        start=(g == 0), stop=(g == PASSES - 1))
+                rows = slice(n * PIECE // PACK, (n + 1) * PIECE // PACK)
+                nc.scalar.copy(by_pairs(a_sb[q, half])[:, :, rows, :],
+                               banks[pb][:, 0:PIECE].rearrange("p (m u e) -> p u m e", u=2, e=2))
+
+        def make_h(q, half, sb, early):
+            terms = (minus_b[q, half], a_sb[q, half]) if early else (a_sb[q, half], minus_b[q, half])
+            difference = transposed_sum(banks[sb], *terms)
             size = passing([P, P, PACK], F32, "size")
-            nc.scalar.activation(size[:], difference[:].rearrange("m t j -> m j t"), ACT.Abs)
-            h = passing([P, P, PACK], BF16, "h")
+            nc.scalar.activation(size[:], difference.rearrange("m t j -> m j t"), ACT.Abs)
+            h = placed([P, P, PACK], BF16, "h%d%d" % (q, half), q) if half == 0 else passing([P, P, PACK], BF16, "h")
             nc.vector.tensor_tensor(h[:], size[:], sens_sb[:, half:half + 1, :].to_broadcast([P, P, PACK]), ALU.mult)
             h_codes[q, half] = held([P, P], U32, "h_codes%d%d" % (q, half))
             h_plane[q, half] = held([P, P], U8, "h_plane%d%d" % (q, half))
             nc.vector.quantize_mx(out=h_codes[q, half][:].bitcast(FP8X4), scales=h_plane[q, half][:],
                                   in_=h[:].rearrange("m j t -> m (j t)"))
 
-        y_sb = {}
+        def make_h_on_scalar(q, half, sb):
+            difference = transposed_sum(banks[sb], a_sb[q, half], minus_b[q, half])
+            size = passing([P, PACK, P], F32, "size")
+            nc.scalar.activation(size[:], difference, ACT.Abs)
+            rows = passing([P, PACK, P], BF16, "h_rows")
+            for t in range(PACK):
+                nc.scalar.activation(rows[:, t, :], size[:, t, :], ACT.Copy, scale=sens_sb[:, half, t:t + 1])
+            h = passing([P, P, PACK], BF16, "h")
+            nc.scalar.copy(h[:], rows[:].rearrange("m t j -> m j t"))
+            h_codes[q, half] = held([P, P], U32, "h_codes%d%d" % (q, half))
+            h_plane[q, half] = held([P, P], U8, "h_plane%d%d" % (q, half))
+            nc.vector.quantize_mx(out=h_codes[q, half][:].bitcast(FP8X4), scales=h_plane[q, half][:],
+                                  in_=h[:].rearrange("m j t -> m (j t)"))
 
-        def make_y(quarters, half):
-            y_sb[quarters, half] = held([P, PACK, P * len(quarters)], F32, "y_sb%d%d" % (quarters[0], half))
-            for place, q in enumerate(quarters):
-                c_sb = passing([P, PACK, P], F32, "c_sb")
-                nc.scalar.copy(by_pairs(c_sb), product(h_operand(q), wc_operand(half)))
-                total = transposed_sum(a_sb[q, half], c_sb)
-                nc.scalar.activation(y_sb[quarters, half][:, :, entries(place)], total[:], ACT.Tanh)
+        def make_y(q, half, into, pb, sb, order=(1, 0)):
+            c_sb = passing([P, PACK, P], F32, "c_sb")
+            nc.scalar.copy(by_pairs(c_sb), product(banks[pb], h_operand(q), wc_operand(half), order))
+            total = transposed_sum(banks[sb], c_sb, a_sb[q, half])
+            nc.scalar.activation(into, total, ACT.Tanh)
 
-        pages = [held([P, T2], F32, "page%d" % t) for t in range(PACK)]
+        def make_y_in_pairs(q, half, into, pb, sbs):
+            c_sb = passing([P, PACK, P], F32, "c_sb")
+            c = product(banks[pb], h_operand(q), wc_operand(half))
+            for u, sb in enumerate(sbs):
+                nc.scalar.copy(by_pairs(c_sb)[:, u], c[:, u])
+            for u, sb in enumerate(sbs):
+                bank = banks[sb][:, 0:2 * P].rearrange("m (e j) -> m e j", e=2)
+                for term in (a_sb[q, half], c_sb):
+                    for e in range(2):
+                        nc.tensor.matmul(bank[:, e, :], lhsT=term[:, 2 * u + e, :], rhs=ident[:], is_transpose=True,
+                                         start=(term is not c_sb and e == 0), stop=(term is c_sb and e == 1))
+                nc.scalar.activation(into[:, 2 * u:2 * u + 2, :], bank, ACT.Tanh)
 
-        def scatter(quarters, half):
-            lo, hi = quarters[0] * P, (quarters[-1] + 1) * P
+        pages = [held([P, T2], F32, "page%d" % t) for t in range(HALVES * PACK)]
+        for t, page in enumerate(pages):
+            (nc.vector if t < 2 else nc.gpsimd).memset(page[:].bitcast(I32), 0)
+
+        def scatter(y, lo, hi, half):
             rows = out[channels(half), :].rearrange("(m t) s -> m t s", t=PACK)
             for t in range(PACK):
-                nc.vector.tensor_tensor(pages[t][:].indirect(offs2_sb[:, lo // GROUP:hi // GROUP]),
-                                        y_sb[quarters, half][:, t, :], wgo_sb[:, lo:hi], ALU.mult)
+                page = pages[half * PACK + t]
+                nc.vector.tensor_tensor(page[:].indirect(offs2_sb[:, lo // GROUP:hi // GROUP]),
+                                        y[:, t, :], wgo_sb[:, lo:hi], ALU.mult)
                 if hi == S:
-                    nc.sync.dma_start(rows[:, t, :], pages[t][:])
+                    nc.sync.dma_start(rows[:, t, :], page[:])
 
-        for half in range(HALVES):
-            for q in range(QUARTERS):
-                make_minus_b(q, half)
-        for q in range(QUARTERS):
-            make_h(q, 0)
-        for q in range(QUARTERS - 1):
-            make_h(q, 1)
-        runs = [(0,), (1,), (2, 3)]
-        make_y(runs[0], 0)
-        make_h(QUARTERS - 1, 1)
-        for run in runs[1:]:
-            make_y(run, 0)
-        for page in pages:
-            nc.vector.memset(page[:].bitcast(I32), 0)
-        for run in runs:
-            scatter(run, 0)
-        whole = tuple(range(QUARTERS))
-        make_y(whole, 1)
-        scatter(whole, 1)
+        def y_tile(quarters, name):
+            return held([P, PACK, quarters * P], F32, name)
+
+        for q, half, bank in ((0, 0, 0), (1, 0, 1), (0, 1, 2), (2, 0, 3), (1, 1, 4), (3, 0, 5)):
+            make_minus_b(q, half, banks[bank])
+        y = {}
+        for q, half in ((0, 0), (0, 1), (1, 0), (1, 1), (2, 0), (3, 0)):
+            y[q, half] = y_tile(1, "y%d%d" % (q, half))
+        make_a(0, 0, 3, True)
+        make_h(0, 0, 0, True)
+        make_a(1, 0, 4, True)
+        make_minus_b(2, 1, banks[6])
+        make_minus_b(3, 1, banks[7])
+        make_a_in_pieces(0, 1, (5, 6))
+        make_h(0, 1, 2, True)
+        make_a(2, 0, 3, True)
+        make_h(1, 0, 1, False)
+        make_y_in_pairs(0, 0, y[0, 0], 3, (4, 0))
+        scatter(y[0, 0], 0, P, 0)
+        make_h(2, 0, 6, False)
+        make_a(1, 1, 5, False)
+        make_h(1, 1, 2, False)
+        make_y(0, 1, y[0, 1][:], 7, 1, (0, 1))
+        scatter(y[0, 1], 0, P, 1)
+        make_a(3, 0, 3, True)
+        make_h(3, 0, 4, False)
+        make_a(2, 1, 7, False)
+        make_h_on_scalar(2, 1, 0)
+        make_y(1, 0, y[1, 0][:], 0, 6)
+        scatter(y[1, 0], P, 2 * P, 0)
+        make_y(1, 1, y[1, 1][:], 0, 2)
+        scatter(y[1, 1], P, 2 * P, 1)
+        make_a(3, 1, 7, False)
+        make_h_on_scalar(3, 1, 4)
+        make_y(2, 0, y[2, 0][:], 6, 5)
+        scatter(y[2, 0], 2 * P, 3 * P, 0)
+        last = y_tile(2, "y_last")
+        make_y(2, 1, last[:, :, entries(0)], 6, 1)
+        make_y(3, 0, y[3, 0][:], 5, 3)
+        scatter(y[3, 0], 3 * P, S, 0)
+        make_y(3, 1, last[:, :, entries(1)], 5, 0)
+        scatter(last, 2 * P, S, 1)

@@ -53,8 +53,9 @@ def tile_list_gamelan_slots_kernel(tc, tab_words, tab_scales, offs, wa, wb_words
         offs_sb = keep.tile([P, S // GROUP], U16, name="offs_sb")
         offs2_sb = keep.tile([P, S // GROUP], U16, name="offs2_sb")
         nc.sync.dma_start(offs_sb[:], offs)
-        wb_sb = held([P, PASSES, 2 * H], U8, "wb_sb")
-        nc.sync.dma_start(wb_sb[:].bitcast(I32), wb_words.rearrange("g p c -> p g c").bitcast(I32))
+        wb_all = held([P, PASSES, 2 * H], U8, "wb_sb")
+        nc.sync.dma_start(wb_all[:].bitcast(I32), wb_words.rearrange("g p c -> p g c").bitcast(I32))
+        wb_sb = [wb_all[:, :, 2 * PASS * half:2 * PASS * (half + 1)] for half in range(HALVES)]
 
         scale_window = [held([P, T], U8, "scale_window%d" % g) for g in range(PASSES)]
         for g in range(PASSES):
@@ -159,7 +160,7 @@ def tile_list_gamelan_slots_kernel(tc, tab_words, tab_scales, offs, wa, wb_words
             return lambda g: (wa_codes[g, half][:].bitcast(FP8X4), wa_plane[g, half][:])
 
         def wb_operand(half):
-            return lambda g: (wb_sb[:, g, 2 * PASS * half:2 * PASS * (half + 1)].bitcast(FP4X4),
+            return lambda g: (wb_sb[half][:, g, :].bitcast(FP4X4),
                               wb_plane[:, g, channels(half)])
 
         def wc_operand(half):
@@ -237,10 +238,11 @@ def tile_list_gamelan_slots_kernel(tc, tab_words, tab_scales, offs, wa, wb_words
             nc.vector.quantize_mx(out=h_codes[q, half][:].bitcast(FP8X4), scales=h_plane[q, half][:],
                                   in_=h[:].rearrange("m j t -> m (j t)"))
 
-        def make_y(q, half, into, pb, sb, order=(1, 0)):
+        def make_y(q, half, into, pb, sb, order=(1, 0), early=False):
             c_sb = passing([P, PACK, P], F32, "c_sb")
             nc.scalar.copy(by_pairs(c_sb), product(banks[pb], h_operand(q), wc_operand(half), order))
-            total = transposed_sum(banks[sb], c_sb, a_sb[q, half])
+            terms = (a_sb[q, half], c_sb) if early else (c_sb, a_sb[q, half])
+            total = transposed_sum(banks[sb], *terms)
             nc.scalar.activation(into, total, ACT.Tanh)
 
         def make_y_in_pairs(q, half, into, pb, sbs):
@@ -293,21 +295,21 @@ def tile_list_gamelan_slots_kernel(tc, tab_words, tab_scales, offs, wa, wb_words
         make_h(1, 1, 2, False)
         make_y(0, 1, y[0, 1][:], 7, 1, (0, 1))
         scatter(y[0, 1], 0, P, 1)
-        make_a(3, 0, 3, True)
-        make_h(3, 0, 4, False)
-        make_a(2, 1, 7, False)
-        make_h_on_scalar(2, 1, 0)
-        make_y(1, 0, y[1, 0][:], 0, 6)
+        make_a(2, 1, 3, False)
+        make_y(1, 0, y[1, 0][:], 5, 6)
         scatter(y[1, 0], P, 2 * P, 0)
-        make_y(1, 1, y[1, 1][:], 0, 2)
+        make_h_on_scalar(2, 1, 4)
+        make_a(3, 0, 7, True)
+        make_h_on_scalar(3, 0, 0)
+        make_y(1, 1, y[1, 1][:], 4, 2)
         scatter(y[1, 1], P, 2 * P, 1)
-        make_a(3, 1, 7, False)
-        make_h_on_scalar(3, 1, 4)
-        make_y(2, 0, y[2, 0][:], 6, 5)
+        make_a(3, 1, 3, False)
+        make_h_on_scalar(3, 1, 1)
+        make_y(2, 0, y[2, 0][:], 2, 1, (0, 1))
         scatter(y[2, 0], 2 * P, 3 * P, 0)
         last = y_tile(2, "y_last")
-        make_y(2, 1, last[:, :, entries(0)], 6, 1)
-        make_y(3, 0, y[3, 0][:], 5, 3)
+        make_y(2, 1, last[:, :, entries(0)], 2, 6)
+        make_y(3, 0, y[3, 0][:], 1, 4, (0, 1), True)
         scatter(y[3, 0], 3 * P, S, 0)
-        make_y(3, 1, last[:, :, entries(1)], 5, 0)
+        make_y(3, 1, last[:, :, entries(1)], 1, 0)
         scatter(last, 2 * P, S, 1)

@@ -186,6 +186,11 @@ def tile_list_gamelan_slots_kernel(tc, tab_words, tab_scales, offs, wa, wb_words
                                      start=(term is first and t == 0), stop=(term is second and t == PACK - 1))
             return bank
 
+        for n in range(4):
+            nc.tensor.matmul_mx(out=banks[7][:], lhsT=wb_sb[0][:, 0, 0:2 * P].bitcast(FP4X4), lhsT_scale=wb_plane[:, 0, 0:P],
+                                rhs=word_window[0][:, 0:PASS].bitcast(FP8X4), rhs_scale=wb_plane[:, 0, 0:PASS],
+                                start=True, stop=True)
+
         a_sb, minus_b = {}, {}
 
         def make_minus_b(q, half, bank):

@@ -48,7 +48,7 @@ def tile_list_gamelan_slots_kernel(tc, tab_words, tab_scales, offs, wa, wb_words
             return ring.tile(shape, dtype, name=name, align_bytes=64)
 
         def placed(shape, dtype, name, kib):
-            return shared.tile(shape, dtype, name=name, align_bytes=64, offset=kib * 1024)
+            return shared.tile(shape, dtype, name=name, align_bytes=64, offset=int(kib * 1024))
 
         offs_sb = keep.tile([P, S // GROUP], U16, name="offs_sb")
         offs2_sb = keep.tile([P, S // GROUP], U16, name="offs2_sb")
@@ -76,6 +76,9 @@ def tile_list_gamelan_slots_kernel(tc, tab_words, tab_scales, offs, wa, wb_words
 
         ident = held([P, P], F32, "ident")
         make_identity(nc, ident[:])
+        pages = [held([P, T2], F32, "page%d" % t) for t in range(PACK)]
+        for t, page in enumerate(pages):
+            (nc.vector if t < 2 else nc.gpsimd).memset(page[:].bitcast(I32), 0)
         sens_sb = held([P, HALVES, PACK], F32, "sens_sb")
         nc.gpsimd.dma_start(sens_sb[:], sens.rearrange("(half m t) -> m half t", half=HALVES, t=PACK))
 
@@ -118,7 +121,7 @@ def tile_list_gamelan_slots_kernel(tc, tab_words, tab_scales, offs, wa, wb_words
 
         load_wc(0)
         wc_plane = held([P, PASSES, H], U8, "wc_plane")
-        nc.gpsimd.memset(wc_plane[:].bitcast(I32), 0)
+        nc.vector.memset(wc_plane[:].bitcast(I32), 0)
         load_plane(wc_plane, wc_scales, [nc.sync] * 4)
 
         load_wc(1)
@@ -132,15 +135,22 @@ def tile_list_gamelan_slots_kernel(tc, tab_words, tab_scales, offs, wa, wb_words
             for g in range(PASSES):
                 wa_codes[g, half] = held([P, PASS], U32, "wa_codes%d%d" % (g, half))
                 wa_plane[g, half] = held([P, PASS], U8, "wa_plane%d%d" % (g, half))
+        grouped = {}
         for g, lo, width in wa_pieces:
-            grouped = held([P, width, PACK], BF16, "wa_grouped%d_%d" % (g, lo))
-            to = grouped[:].rearrange("p (c e) i -> p c i e", e=LINE)
-            source = wa_raw[g, lo][:].rearrange("p i (c e) -> p c i e", e=LINE)
-            nc.vector.tensor_copy(to, source)
-            half, columns = lo // PASS, slice(lo % PASS, lo % PASS + width)
+            half, first = lo // PASS, lo % PASS
+            if first == 0:
+                grouped[g, half] = held([P, PASS, PACK], BF16, "wa_grouped%d%d" % (g, half))
+            nc.vector.tensor_copy(grouped[g, half][:, first:first + width, :].rearrange("p (c e) i -> p c i e", e=LINE),
+                                  wa_raw[g, lo][:].rearrange("p i (c e) -> p c i e", e=LINE))
+            if (g, half) == (PASSES - 1, HALVES - 1):
+                columns = slice(first, first + width)
+            elif first + width == PASS:
+                columns = slice(0, PASS)
+            else:
+                continue
             nc.vector.quantize_mx(out=wa_codes[g, half][:, columns].bitcast(FP8X4),
                                   scales=wa_plane[g, half][:, columns],
-                                  in_=grouped[:].rearrange("p c i -> p (c i)"))
+                                  in_=grouped[g, half][:, columns, :].rearrange("p c i -> p (c i)"))
 
         h_codes, h_plane = {}, {}
 
@@ -244,28 +254,25 @@ def tile_list_gamelan_slots_kernel(tc, tab_words, tab_scales, offs, wa, wb_words
                                   in_=h[:].rearrange("m j t -> m (j t)"))
 
         def make_y(q, half, into, pb, sb, order=(1, 0), early=False):
-            c_sb = passing([P, PACK, P], F32, "c_sb")
+            c_sb = placed([P, PACK, P], F32, "c_01", 15) if (q, half) == (0, 1) else passing([P, PACK, P], F32, "c_sb")
             nc.scalar.copy(by_pairs(c_sb), product(banks[pb], h_operand(q), wc_operand(half), order))
             terms = (a_sb[q, half], c_sb) if early else (c_sb, a_sb[q, half])
             total = transposed_sum(banks[sb], *terms)
             nc.scalar.activation(into, total, ACT.Tanh)
 
         def make_y_in_pairs(q, half, into, pb, sbs):
-            c_sb = passing([P, PACK, P], F32, "c_sb")
+            c_pairs = [held([P, 2, P], F32, "c_pair0"), placed([P, 2, P], F32, "c_pair1", 7.5)]
             c = product(banks[pb], h_operand(q), wc_operand(half))
-            for u, sb in enumerate(sbs):
-                nc.scalar.copy(by_pairs(c_sb)[:, u], c[:, u])
+            for u in range(2):
+                nc.scalar.copy(c_pairs[u][:].rearrange("p e m -> p m e"), c[:, u])
             for u, sb in enumerate(sbs):
                 bank = banks[sb][:, 0:2 * P].rearrange("m (e j) -> m e j", e=2)
-                for term in (a_sb[q, half], c_sb):
+                for n, term in enumerate((a_sb[q, half][:, 2 * u:2 * u + 2, :], c_pairs[u])):
                     for e in range(2):
-                        nc.tensor.matmul(bank[:, e, :], lhsT=term[:, 2 * u + e, :], rhs=ident[:], is_transpose=True,
-                                         start=(term is not c_sb and e == 0), stop=(term is c_sb and e == 1))
+                        nc.tensor.matmul(bank[:, e, :], lhsT=term[:, e, :], rhs=ident[:], is_transpose=True,
+                                         start=(n == 0 and e == 0), stop=(n == 1 and e == 1))
                 nc.scalar.activation(into[:, 2 * u:2 * u + 2, :], bank, ACT.Tanh)
 
-        pages = [held([P, T2], F32, "page%d" % t) for t in range(HALVES * PACK)]
-        for t, page in enumerate(pages):
-            (nc.vector if t < 2 else nc.gpsimd).memset(page[:].bitcast(I32), 0)
 
         def scatter(y, lo, hi, half):
             rows = out[channels(half), :].rearrange("(m t) s -> m t s", t=PACK)
@@ -299,15 +306,18 @@ def tile_list_gamelan_slots_kernel(tc, tab_words, tab_scales, offs, wa, wb_words
         make_a(1, 1, 5, False)
         make_h(1, 1, 2, False)
         make_y(0, 1, y[0, 1][:], 7, 1, (0, 1))
+        for t in range(PACK):
+            pages.append(placed([P, T2], F32, "page%d" % (PACK + t), 4 + 4 * t))
+            nc.gpsimd.memset(pages[-1][:].bitcast(I32), 0)
         scatter(y[0, 1], 0, P, 1)
         make_a(2, 1, 3, False)
-        make_y(1, 0, y[1, 0][:], 5, 6)
-        scatter(y[1, 0], P, 2 * P, 0)
         make_h_on_scalar(2, 1, 4)
+        make_y(1, 0, y[1, 0][:], 4, 6, (0, 1), True)
+        scatter(y[1, 0], P, 2 * P, 0)
         make_a(3, 0, 7, True)
-        make_h_on_scalar(3, 0, 0)
         make_y(1, 1, y[1, 1][:], 4, 2)
         scatter(y[1, 1], P, 2 * P, 1)
+        make_h_on_scalar(3, 0, 0)
         make_a(3, 1, 3, False)
         make_h_on_scalar(3, 1, 1)
         make_y(2, 0, y[2, 0][:], 2, 1, (0, 1))

@@ -48,7 +48,7 @@ def tile_list_gamelan_slots_kernel(tc, tab_words, tab_scales, offs, wa, wb_words
             return ring.tile(shape, dtype, name=name, align_bytes=64)
 
         def placed(shape, dtype, name, kib):
-            return shared.tile(shape, dtype, name=name, align_bytes=64, offset=int(kib * 1024))
+            return shared.tile(shape, dtype, name=name, align_bytes=64, offset=kib * 1024)
 
         offs_sb = keep.tile([P, S // GROUP], U16, name="offs_sb")
         offs2_sb = keep.tile([P, S // GROUP], U16, name="offs2_sb")
@@ -72,19 +72,17 @@ def tile_list_gamelan_slots_kernel(tc, tab_words, tab_scales, offs, wa, wb_words
                 queue.dma_start(plane[r:P:QUADRANT].bitcast(I32),
                                 scales[:, r:16:4, :].rearrange("g d c -> d g c").bitcast(I32))
 
-        load_plane(wb_plane, wb_scales, [nc.sync] * 4)
 
         ident = held([P, P], F32, "ident")
         make_identity(nc, ident[:])
-        pages = [held([P, T2], F32, "page%d" % t) for t in range(PACK)]
-        for t, page in enumerate(pages):
-            (nc.vector if t < 2 else nc.gpsimd).memset(page[:].bitcast(I32), 0)
         sens_sb = held([P, HALVES, PACK], F32, "sens_sb")
         nc.gpsimd.dma_start(sens_sb[:], sens.rearrange("(half m t) -> m half t", half=HALVES, t=PACK))
 
         word_window = [held([P, T], I32, "word_window%d" % g) for g in range(PASSES)]
         for g in range(PASSES):
             nc.sync.dma_start(word_window[g][:], tab_words[g].rearrange("p t i -> p (t i)").bitcast(I32))
+            if g == 0:
+                load_plane(wb_plane, wb_scales, [nc.sync] * 4)
 
         v_scale = held([P, PASSES, S], U8, "v_scale")
         for g in range(PASSES):
@@ -105,6 +103,8 @@ def tile_list_gamelan_slots_kernel(tc, tab_words, tab_scales, offs, wa, wb_words
         for half, g in ((0, 1), (1, 0), (1, 1)):
             for lo in range(0, PASS, PIECE):
                 wa_pieces.append((g, half * PASS + lo, PIECE))
+        g, lo, width = wa_pieces.pop()
+        wa_pieces.extend([(g, lo, width // 2), (g, lo + width // 2, width // 2)])
         wa_raw = {}
         for g, lo, width in wa_pieces:
             name = "wa_raw%d_%d" % (g, lo)
@@ -121,7 +121,7 @@ def tile_list_gamelan_slots_kernel(tc, tab_words, tab_scales, offs, wa, wb_words
 
         load_wc(0)
         wc_plane = held([P, PASSES, H], U8, "wc_plane")
-        nc.vector.memset(wc_plane[:].bitcast(I32), 0)
+        nc.gpsimd.memset(wc_plane[:].bitcast(I32), 0)
         load_plane(wc_plane, wc_scales, [nc.sync] * 4)
 
         load_wc(1)
@@ -231,9 +231,13 @@ def tile_list_gamelan_slots_kernel(tc, tab_words, tab_scales, offs, wa, wb_words
             terms = (minus_b[q, half], a_sb[q, half]) if early else (a_sb[q, half], minus_b[q, half])
             difference = transposed_sum(banks[sb], *terms)
             size = passing([P, P, PACK], F32, "size")
-            nc.scalar.activation(size[:], difference.rearrange("m t j -> m j t"), ACT.Abs)
-            h = placed([P, P, PACK], BF16, "h%d%d" % (q, half), q) if half == 0 else passing([P, P, PACK], BF16, "h")
-            nc.vector.tensor_tensor(h[:], size[:], sens_sb[:, half:half + 1, :].to_broadcast([P, P, PACK]), ALU.mult)
+            parts = (slice(0, P // 2), slice(P // 2, P)) if (q, half) == (0, 1) else (slice(0, P),)
+            for part in parts:
+                nc.scalar.activation(size[:, part, :], difference.rearrange("m t j -> m j t")[:, part, :], ACT.Abs)
+            h = placed([P, P, PACK], BF16, "h%d%d" % (q, half), q % 2) if half == 0 and q < 2 else passing([P, P, PACK], BF16, "h")
+            for part in parts:
+                nc.vector.tensor_tensor(h[:, part, :], size[:, part, :], sens_sb[:, half:half + 1, :].to_broadcast(
+                    [P, part.stop - part.start, PACK]), ALU.mult)
             h_codes[q, half] = held([P, P], U32, "h_codes%d%d" % (q, half))
             h_plane[q, half] = held([P, P], U8, "h_plane%d%d" % (q, half))
             nc.vector.quantize_mx(out=h_codes[q, half][:].bitcast(FP8X4), scales=h_plane[q, half][:],
@@ -254,25 +258,28 @@ def tile_list_gamelan_slots_kernel(tc, tab_words, tab_scales, offs, wa, wb_words
                                   in_=h[:].rearrange("m j t -> m (j t)"))
 
         def make_y(q, half, into, pb, sb, order=(1, 0), early=False):
-            c_sb = placed([P, PACK, P], F32, "c_01", 15) if (q, half) == (0, 1) else passing([P, PACK, P], F32, "c_sb")
+            c_sb = passing([P, PACK, P], F32, "c_sb")
             nc.scalar.copy(by_pairs(c_sb), product(banks[pb], h_operand(q), wc_operand(half), order))
             terms = (a_sb[q, half], c_sb) if early else (c_sb, a_sb[q, half])
             total = transposed_sum(banks[sb], *terms)
             nc.scalar.activation(into, total, ACT.Tanh)
 
         def make_y_in_pairs(q, half, into, pb, sbs):
-            c_pairs = [held([P, 2, P], F32, "c_pair0"), placed([P, 2, P], F32, "c_pair1", 7.5)]
+            c_sb = passing([P, PACK, P], F32, "c_sb")
             c = product(banks[pb], h_operand(q), wc_operand(half))
-            for u in range(2):
-                nc.scalar.copy(c_pairs[u][:].rearrange("p e m -> p m e"), c[:, u])
+            for u, sb in enumerate(sbs):
+                nc.scalar.copy(by_pairs(c_sb)[:, u], c[:, u])
             for u, sb in enumerate(sbs):
                 bank = banks[sb][:, 0:2 * P].rearrange("m (e j) -> m e j", e=2)
-                for n, term in enumerate((a_sb[q, half][:, 2 * u:2 * u + 2, :], c_pairs[u])):
+                for term in (a_sb[q, half], c_sb):
                     for e in range(2):
-                        nc.tensor.matmul(bank[:, e, :], lhsT=term[:, e, :], rhs=ident[:], is_transpose=True,
-                                         start=(n == 0 and e == 0), stop=(n == 1 and e == 1))
+                        nc.tensor.matmul(bank[:, e, :], lhsT=term[:, 2 * u + e, :], rhs=ident[:], is_transpose=True,
+                                         start=(term is not c_sb and e == 0), stop=(term is c_sb and e == 1))
                 nc.scalar.activation(into[:, 2 * u:2 * u + 2, :], bank, ACT.Tanh)
 
+        pages = [held([P, T2], F32, "page%d" % t) for t in range(HALVES * PACK)]
+        for t, page in enumerate(pages):
+            (nc.vector if t < 2 else nc.gpsimd).memset(page[:].bitcast(I32), 0)
 
         def scatter(y, lo, hi, half):
             rows = out[channels(half), :].rearrange("(m t) s -> m t s", t=PACK)
@@ -306,9 +313,6 @@ def tile_list_gamelan_slots_kernel(tc, tab_words, tab_scales, offs, wa, wb_words
         make_a(1, 1, 5, False)
         make_h(1, 1, 2, False)
         make_y(0, 1, y[0, 1][:], 7, 1, (0, 1))
-        for t in range(PACK):
-            pages.append(placed([P, T2], F32, "page%d" % (PACK + t), 4 + 4 * t))
-            nc.gpsimd.memset(pages[-1][:].bitcast(I32), 0)
         scatter(y[0, 1], 0, P, 1)
         make_a(2, 1, 3, False)
         make_h_on_scalar(2, 1, 4)
@@ -320,10 +324,10 @@ def tile_list_gamelan_slots_kernel(tc, tab_words, tab_scales, offs, wa, wb_words
         make_h_on_scalar(3, 0, 0)
         make_a(3, 1, 3, False)
         make_h_on_scalar(3, 1, 1)
-        make_y(2, 0, y[2, 0][:], 2, 1, (0, 1))
+        make_y(2, 0, y[2, 0][:], 6, 1, (0, 1))
         scatter(y[2, 0], 2 * P, 3 * P, 0)
         last = y_tile(2, "y_last")
-        make_y(2, 1, last[:, :, entries(0)], 2, 6)
+        make_y(2, 1, last[:, :, entries(0)], 6, 2)
         make_y(3, 0, y[3, 0][:], 1, 4, (0, 1), True)
         scatter(y[3, 0], 3 * P, S, 0)
         make_y(3, 1, last[:, :, entries(1)], 1, 0)

@@ -22,18 +22,28 @@ PACK = 4
 PASS = P * PACK
 PASSES = K // PASS
 HALVES = H // PASS
-QUARTERS = S // P
 QUADRANT = 32
+SCALE_ROWS = 4
 BLOCK_PARTITIONS = 8
 GROUP = 16
 LINE = 4
-BANKS = 4
+BANKS = 8
 PIECE = 256
 DEPTH = 3
+WARM_UPS = 4
+VECTOR_PAGES = 2
+KIB = 1024
+
+LAST_PIECE = 0
+LAST_CODES = 2
+LAST_ROWS = 4
+
+FIRST_PASS_FIRST = (0, 1)
+LAST_PASS_FIRST = (1, 0)
 
 
 def tile_list_gamelan_slots_kernel(tc, tab_words, tab_scales, offs, wa, wb_words, wb_scales, sens,
-                                             wc_words, wc_scales, wgo, offs2, out):
+                                                wc_words, wc_scales, wgo, offs2, out):
     nc = tc.nc
     with ExitStack() as ctx:
         keep = ctx.enter_context(tc.tile_pool(name="keep", bufs=1))
@@ -47,15 +57,14 @@ def tile_list_gamelan_slots_kernel(tc, tab_words, tab_scales, offs, wa, wb_words
         def passing(shape, dtype, name):
             return ring.tile(shape, dtype, name=name, align_bytes=64)
 
-        def placed(shape, dtype, name, kib):
-            return shared.tile(shape, dtype, name=name, align_bytes=64, offset=kib * 1024)
+        def placed(shape, dtype, name, place):
+            return shared.tile(shape, dtype, name=name, align_bytes=64, offset=place * KIB)
 
         offs_sb = keep.tile([P, S // GROUP], U16, name="offs_sb")
         offs2_sb = keep.tile([P, S // GROUP], U16, name="offs2_sb")
         nc.sync.dma_start(offs_sb[:], offs)
-        wb_all = held([P, PASSES, 2 * H], U8, "wb_sb")
-        nc.sync.dma_start(wb_all[:].bitcast(I32), wb_words.rearrange("g p c -> p g c").bitcast(I32))
-        wb_sb = [wb_all[:, :, 2 * PASS * half:2 * PASS * (half + 1)] for half in range(HALVES)]
+        wb_sb = held([P, PASSES, 2 * H], U8, "wb_sb")
+        nc.sync.dma_start(wb_sb[:].bitcast(I32), wb_words.rearrange("g p c -> p g c").bitcast(I32))
 
         scale_window = [held([P, T], U8, "scale_window%d" % g) for g in range(PASSES)]
         for g in range(PASSES):
@@ -67,11 +76,10 @@ def tile_list_gamelan_slots_kernel(tc, tab_words, tab_scales, offs, wa, wb_words
         nc.vector.memset(v_plane[:].bitcast(I32), 0)
         nc.gpsimd.memset(wb_plane[:].bitcast(I32), 0)
 
-        def load_plane(plane, scales, queues):
-            for r, queue in enumerate(queues):
-                queue.dma_start(plane[r:P:QUADRANT].bitcast(I32),
-                                scales[:, r:16:4, :].rearrange("g d c -> d g c").bitcast(I32))
-
+        def load_plane(plane, scales):
+            for r in range(SCALE_ROWS):
+                nc.sync.dma_start(plane[r:P:QUADRANT].bitcast(I32),
+                                  scales[:, r::SCALE_ROWS, :].rearrange("g d c -> d g c").bitcast(I32))
 
         ident = held([P, P], F32, "ident")
         make_identity(nc, ident[:])
@@ -79,39 +87,39 @@ def tile_list_gamelan_slots_kernel(tc, tab_words, tab_scales, offs, wa, wb_words
         nc.gpsimd.dma_start(sens_sb[:], sens.rearrange("(half m t) -> m half t", half=HALVES, t=PACK))
 
         word_window = [held([P, T], I32, "word_window%d" % g) for g in range(PASSES)]
-        for g in range(PASSES):
+
+        def load_words(g):
             nc.sync.dma_start(word_window[g][:], tab_words[g].rearrange("p t i -> p (t i)").bitcast(I32))
-            if g == 0:
-                load_plane(wb_plane, wb_scales, [nc.sync] * 4)
+
+        load_words(0)
+        load_plane(wb_plane, wb_scales)
+        load_words(1)
 
         v_scale = held([P, PASSES, S], U8, "v_scale")
         for g in range(PASSES):
             nc.vector.tensor_copy(v_scale[:, g, :], scale_window[g][:].indirect(offs_sb[:]))
-        for r in range(4):
+        for r in range(SCALE_ROWS):
             nc.sync.dma_start(v_plane[r:P:QUADRANT].rearrange("p g j -> p (g j)").bitcast(I32),
                               v_scale[BLOCK_PARTITIONS * r:P:QUADRANT].rearrange("p g j -> p (g j)").bitcast(I32))
 
         v_codes = [held([P, S], U32, "v_codes%d" % g) for g in range(PASSES)]
         for g in range(PASSES):
-            width = S if g == 0 else S // 2
-            for lo in range(0, S, width):
-                nc.vector.tensor_copy(v_codes[g][:, lo:lo + width], word_window[g][:].bitcast(U32).indirect(
-                    offs_sb[:, lo // GROUP:(lo + width) // GROUP]))
+            length = S // 2 if g == PASSES - 1 else S
+            for lo in range(0, S, length):
+                nc.vector.tensor_copy(v_codes[g][:, lo:lo + length], word_window[g][:].bitcast(U32).indirect(
+                    offs_sb[:, lo // GROUP:(lo + length) // GROUP]))
 
-        wa_pieces = []
-        wa_pieces.append((0, 0, PASS))
+        wa_pieces = [(0, 0, PASS)]
         for half, g in ((0, 1), (1, 0), (1, 1)):
-            for lo in range(0, PASS, PIECE):
-                wa_pieces.append((g, half * PASS + lo, PIECE))
-        g, lo, width = wa_pieces.pop()
-        wa_pieces.extend([(g, lo, width // 2), (g, lo + width // 2, width // 2)])
+            wa_pieces.extend((g, half * PASS + lo, PIECE) for lo in range(0, PASS, PIECE))
+        wa_pieces = wa_pieces[:-1] + [(PASSES - 1, H - PIECE + lo, PIECE // 2) for lo in (0, PIECE // 2)]
         wa_raw = {}
         for g, lo, width in wa_pieces:
-            name = "wa_raw%d_%d" % (g, lo)
-            last = (g, lo, width) == wa_pieces[-1]
-            wa_raw[g, lo] = placed([P, PACK, width], F32, name, 0) if last else held([P, PACK, width], F32, name)
-            rows = wa[g * PASS:(g + 1) * PASS, lo:lo + width]
-            nc.sync.dma_start(wa_raw[g, lo][:], rows.rearrange("(p i) c -> p i c", i=PACK))
+            shape, name = [P, PACK, width], "wa_raw%d_%d" % (g, lo)
+            wa_raw[g, lo] = placed(shape, F32, name, LAST_PIECE) if lo + width == H and g == PASSES - 1 \
+                else held(shape, F32, name)
+            piece = wa[g * PASS:(g + 1) * PASS, lo:lo + width]
+            nc.sync.dma_start(wa_raw[g, lo][:], piece.rearrange("(p i) c -> p i c", i=PACK))
 
         wc_sb = [held([P, PASSES, PASS], I32, "wc_sb%d" % half) for half in range(HALVES)]
 
@@ -122,35 +130,33 @@ def tile_list_gamelan_slots_kernel(tc, tab_words, tab_scales, offs, wa, wb_words
         load_wc(0)
         wc_plane = held([P, PASSES, H], U8, "wc_plane")
         nc.gpsimd.memset(wc_plane[:].bitcast(I32), 0)
-        load_plane(wc_plane, wc_scales, [nc.sync] * 4)
-
+        load_plane(wc_plane, wc_scales)
         load_wc(1)
         wgo_sb = held([P, S], F32, "wgo_sb")
         nc.sync.dma_start(wgo_sb[:], wgo)
         nc.sync.dma_start(offs2_sb[:], offs2)
 
-
-        wa_codes, wa_plane = {}, {}
+        wa_codes, wa_plane, wa_grouped = {}, {}, {}
         for half in range(HALVES):
             for g in range(PASSES):
                 wa_codes[g, half] = held([P, PASS], U32, "wa_codes%d%d" % (g, half))
                 wa_plane[g, half] = held([P, PASS], U8, "wa_plane%d%d" % (g, half))
-        grouped = {}
         for g, lo, width in wa_pieces:
-            half, first = lo // PASS, lo % PASS
-            if first == 0:
-                grouped[g, half] = held([P, PASS, PACK], BF16, "wa_grouped%d%d" % (g, half))
-            nc.vector.tensor_copy(grouped[g, half][:, first:first + width, :].rearrange("p (c e) i -> p c i e", e=LINE),
-                                  wa_raw[g, lo][:].rearrange("p i (c e) -> p c i e", e=LINE))
-            if (g, half) == (PASSES - 1, HALVES - 1):
-                columns = slice(first, first + width)
-            elif first + width == PASS:
-                columns = slice(0, PASS)
-            else:
-                continue
-            nc.vector.quantize_mx(out=wa_codes[g, half][:, columns].bitcast(FP8X4),
-                                  scales=wa_plane[g, half][:, columns],
-                                  in_=grouped[g, half][:, columns, :].rearrange("p c i -> p (c i)"))
+            half, column = divmod(lo, PASS)
+            if column == 0:
+                wa_grouped[g, half] = held([P, PASS, PACK], BF16, "wa_grouped%d%d" % (g, half))
+            to = wa_grouped[g, half][:, column:column + width, :].rearrange("p (c e) i -> p c i e", e=LINE)
+            source = wa_raw[g, lo][:].rearrange("p i (c e) -> p c i e", e=LINE)
+            if width > PIECE:
+                share = (width - PIECE) // LINE
+                nc.scalar.activation(to[:, 0:share], source[:, 0:share], ACT.Copy)
+                to, source = to[:, share:], source[:, share:]
+            nc.vector.tensor_copy(to, source)
+            if half == HALVES - 1 or column + width == PASS:
+                columns = slice(column if half == HALVES - 1 else 0, column + width)
+                nc.vector.quantize_mx(out=wa_codes[g, half][:, columns].bitcast(FP8X4),
+                                      scales=wa_plane[g, half][:, columns],
+                                      in_=wa_grouped[g, half][:, columns, :].rearrange("p c i -> p (c i)"))
 
         h_codes, h_plane = {}, {}
 
@@ -166,169 +172,180 @@ def tile_list_gamelan_slots_kernel(tc, tab_words, tab_scales, offs, wa, wb_words
         def h_operand(q):
             return lambda g: (h_codes[q, g][:].bitcast(FP8X4), h_plane[q, g][:])
 
-        def wa_operand(half):
-            return lambda g: (wa_codes[g, half][:].bitcast(FP8X4), wa_plane[g, half][:])
+        def wa_operand(half, columns=slice(0, PASS)):
+            return lambda g: (wa_codes[g, half][:, columns].bitcast(FP8X4), wa_plane[g, half][:, columns])
 
         def wb_operand(half):
-            return lambda g: (wb_sb[half][:, g, :].bitcast(FP4X4),
+            return lambda g: (wb_sb[:, g, 2 * PASS * half:2 * PASS * (half + 1)].bitcast(FP4X4),
                               wb_plane[:, g, channels(half)])
 
         def wc_operand(half):
             return lambda g: (wc_sb[half][:, g, :].bitcast(FP8X4), wc_plane[:, g, channels(half)])
 
-        banks = [psum.tile([P, PASS], F32, name="bank%d" % i) for i in range(2 * BANKS)]
+        banks = [psum.tile([P, PASS], F32, name="bank%d" % n) for n in range(BANKS)]
+        bank_of = {}
 
-        def product(bank, stationary, moving, order=(0, 1)):
+        def take(step, after):
+            bank_of[step] = bank_of[after]
+            return bank_of[step]
+
+        def product(into, stationary, moving, order):
             for g in order:
                 (lhs, lhs_scale), (rhs, rhs_scale) = stationary(g), moving(g)
-                nc.tensor.matmul_mx(out=bank[:], lhsT=lhs, lhsT_scale=lhs_scale, rhs=rhs, rhs_scale=rhs_scale,
+                nc.tensor.matmul_mx(out=into, lhsT=lhs, lhsT_scale=lhs_scale, rhs=rhs, rhs_scale=rhs_scale,
                                     start=(g == order[0]), stop=(g == order[-1]))
-            return bank[:].rearrange("p (m u e) -> p u m e", u=2, e=2)
+            return into.rearrange("p (m u e) -> p u m e", u=2, e=2)
 
         def by_pairs(tile):
             return tile[:].rearrange("p (u e) m -> p u m e", e=2)
 
         def transposed_sum(bank, first, second):
-            bank = bank[:].rearrange("m (t j) -> m t j", t=PACK)
-            for term in (first, second):
-                for t in range(PACK):
-                    nc.tensor.matmul(bank[:, t, :], lhsT=term[:, t, :], rhs=ident[:], is_transpose=True,
-                                     start=(term is first and t == 0), stop=(term is second and t == PACK - 1))
-            return bank
+            count = first.shape[1]
+            total = bank[:, 0:count * P].rearrange("m (t j) -> m t j", t=count)
+            for n, term in enumerate((first, second)):
+                for t in range(count):
+                    nc.tensor.matmul(total[:, t, :], lhsT=term[:, t, :], rhs=ident[:], is_transpose=True,
+                                     start=(n == 0 and t == 0), stop=(n == 1 and t == count - 1))
+            return total
 
-        for n in range(4):
-            nc.tensor.matmul_mx(out=banks[7][:], lhsT=wb_sb[0][:, 0, 0:2 * P].bitcast(FP4X4), lhsT_scale=wb_plane[:, 0, 0:P],
-                                rhs=word_window[0][:, 0:PASS].bitcast(FP8X4), rhs_scale=wb_plane[:, 0, 0:PASS],
-                                start=True, stop=True)
+        for n in range(WARM_UPS):
+            nc.tensor.matmul_mx(out=banks[-1][:], lhsT=wb_sb[:, 0, 0:2 * P].bitcast(FP4X4),
+                                lhsT_scale=wb_plane[:, 0, 0:P], rhs=word_window[0][:, 0:PASS].bitcast(FP8X4),
+                                rhs_scale=wb_plane[:, 0, 0:PASS], start=True, stop=True)
 
         a_sb, minus_b = {}, {}
 
-        def make_minus_b(q, half, bank):
+        def make_minus_b(q, half):
+            bank = banks[len(minus_b)]
+            bank_of["b%d%d" % (q, half)] = bank
             minus_b[q, half] = held([P, PACK, P], F32, "minus_b%d%d" % (q, half))
-            nc.scalar.activation(by_pairs(minus_b[q, half]), product(bank, v_operand(q), wb_operand(half)),
-                                 ACT.Copy, scale=-1.0)
+            b = product(bank[:], v_operand(q), wb_operand(half), FIRST_PASS_FIRST)
+            nc.scalar.activation(by_pairs(minus_b[q, half]), b, ACT.Copy, scale=-1.0)
 
-        def make_a(q, half, pb, early):
+        def make_a(q, half, after):
             a_sb[q, half] = held([P, PACK, P], F32, "a_sb%d%d" % (q, half))
-            nc.scalar.copy(by_pairs(a_sb[q, half]),
-                           product(banks[pb], v_operand(q), wa_operand(half), (0, 1) if early else (1, 0)))
+            order = FIRST_PASS_FIRST if half == 0 else LAST_PASS_FIRST
+            a = product(take("a%d%d" % (q, half), after)[:], v_operand(q), wa_operand(half), order)
+            nc.scalar.copy(by_pairs(a_sb[q, half]), a)
 
-        def make_a_in_pieces(q, half, pbs):
+        def make_a_by_pieces(q, half, after):
             a_sb[q, half] = held([P, PACK, P], F32, "a_sb%d%d" % (q, half))
-            for n, pb in enumerate(pbs):
-                columns = slice(n * PIECE, (n + 1) * PIECE)
-                for g in range(PASSES):
-                    lhs, lhs_scale = v_operand(q)(g)
-                    nc.tensor.matmul_mx(out=banks[pb][:, 0:PIECE], lhsT=lhs, lhsT_scale=lhs_scale,
-                                        rhs=wa_codes[g, half][:, columns].bitcast(FP8X4),
-                                        rhs_scale=wa_plane[g, half][:, columns],
-                                        start=(g == 0), stop=(g == PASSES - 1))
-                rows = slice(n * PIECE // PACK, (n + 1) * PIECE // PACK)
-                nc.scalar.copy(by_pairs(a_sb[q, half])[:, :, rows, :],
-                               banks[pb][:, 0:PIECE].rearrange("p (m u e) -> p u m e", u=2, e=2))
+            for n in range(PASS // PIECE):
+                bank = take("a%d%d_%d" % (q, half, n), after[n])
+                a = product(bank[:, 0:PIECE], v_operand(q), wa_operand(half, slice(n * PIECE, (n + 1) * PIECE)),
+                            FIRST_PASS_FIRST)
+                nc.scalar.copy(by_pairs(a_sb[q, half])[:, :, n * PIECE // PACK:(n + 1) * PIECE // PACK, :], a)
 
-        def make_h(q, half, sb, early):
-            terms = (minus_b[q, half], a_sb[q, half]) if early else (a_sb[q, half], minus_b[q, half])
-            difference = transposed_sum(banks[sb], *terms)
+        def difference(q, half, after, b_first):
+            terms = (minus_b[q, half], a_sb[q, half]) if b_first else (a_sb[q, half], minus_b[q, half])
+            return transposed_sum(take("h%d%d" % (q, half), after), *terms)
+
+        def quantise_h(q, half, h, codes=None):
+            h_codes[q, half] = held([P, P], U32, "h_codes%d%d" % (q, half)) if codes is None else codes
+            h_plane[q, half] = held([P, P], U8, "h_plane%d%d" % (q, half))
+            nc.vector.quantize_mx(out=h_codes[q, half][:].bitcast(FP8X4), scales=h_plane[q, half][:],
+                                  in_=h[:].rearrange("m j t -> m (j t)"))
+
+        def make_h(q, half, after, b_first=False, parts=1, place=None):
+            total = difference(q, half, after, b_first).rearrange("m t j -> m j t")
             size = passing([P, P, PACK], F32, "size")
-            parts = (slice(0, P // 2), slice(P // 2, P)) if (q, half) == (0, 1) else (slice(0, P),)
-            for part in parts:
-                nc.scalar.activation(size[:, part, :], difference.rearrange("m t j -> m j t")[:, part, :], ACT.Abs)
-            h = placed([P, P, PACK], BF16, "h%d%d" % (q, half), q % 2) if half == 0 and q < 2 else passing([P, P, PACK], BF16, "h")
-            for part in parts:
-                nc.vector.tensor_tensor(h[:, part, :], size[:, part, :], sens_sb[:, half:half + 1, :].to_broadcast(
-                    [P, part.stop - part.start, PACK]), ALU.mult)
-            h_codes[q, half] = held([P, P], U32, "h_codes%d%d" % (q, half))
-            h_plane[q, half] = held([P, P], U8, "h_plane%d%d" % (q, half))
-            nc.vector.quantize_mx(out=h_codes[q, half][:].bitcast(FP8X4), scales=h_plane[q, half][:],
-                                  in_=h[:].rearrange("m j t -> m (j t)"))
+            runs = [slice(lo, lo + P // parts) for lo in range(0, P, P // parts)]
+            for run in runs:
+                nc.scalar.activation(size[:, run, :], total[:, run, :], ACT.Abs)
+            h = passing([P, P, PACK], BF16, "h") if place is None \
+                else placed([P, P, PACK], BF16, "h%d%d" % (q, half), place)
+            factor = sens_sb[:, half:half + 1, :].to_broadcast([P, P // parts, PACK])
+            for run in runs:
+                nc.vector.tensor_tensor(h[:, run, :], size[:, run, :], factor, ALU.mult)
+            quantise_h(q, half, h)
 
-        def make_h_on_scalar(q, half, sb):
-            difference = transposed_sum(banks[sb], a_sb[q, half], minus_b[q, half])
+        def scale_on_scalar(q, half, after, place=None):
+            total = difference(q, half, after, False)
             size = passing([P, PACK, P], F32, "size")
-            nc.scalar.activation(size[:], difference, ACT.Abs)
-            rows = passing([P, PACK, P], BF16, "h_rows")
+            nc.scalar.activation(size[:], total, ACT.Abs)
+            h_rows = passing([P, PACK, P], BF16, "h_rows") if place is None \
+                else placed([P, PACK, P], BF16, "h_rows%d%d" % (q, half), place)
             for t in range(PACK):
-                nc.scalar.activation(rows[:, t, :], size[:, t, :], ACT.Copy, scale=sens_sb[:, half, t:t + 1])
+                nc.scalar.activation(h_rows[:, t, :], size[:, t, :], ACT.Copy, scale=sens_sb[:, half, t:t + 1])
             h = passing([P, P, PACK], BF16, "h")
-            nc.scalar.copy(h[:], rows[:].rearrange("m t j -> m j t"))
-            h_codes[q, half] = held([P, P], U32, "h_codes%d%d" % (q, half))
-            h_plane[q, half] = held([P, P], U8, "h_plane%d%d" % (q, half))
-            nc.vector.quantize_mx(out=h_codes[q, half][:].bitcast(FP8X4), scales=h_plane[q, half][:],
-                                  in_=h[:].rearrange("m j t -> m (j t)"))
+            nc.scalar.copy(h[:], h_rows[:].rearrange("m t j -> m j t"))
+            return h
 
-        def make_y(q, half, into, pb, sb, order=(1, 0), early=False):
-            c_sb = passing([P, PACK, P], F32, "c_sb")
-            nc.scalar.copy(by_pairs(c_sb), product(banks[pb], h_operand(q), wc_operand(half), order))
-            terms = (a_sb[q, half], c_sb) if early else (c_sb, a_sb[q, half])
-            total = transposed_sum(banks[sb], *terms)
-            nc.scalar.activation(into, total, ACT.Tanh)
+        def make_y(q, half, into, c_after, y_after, order=LAST_PASS_FIRST, a_first=False, place=None):
+            c_sb = passing([P, PACK, P], F32, "c_sb") if place is None \
+                else placed([P, PACK, P], F32, "c_sb%d%d" % (q, half), place)
+            c = product(take("c%d%d" % (q, half), c_after)[:], h_operand(q), wc_operand(half), order)
+            nc.scalar.copy(by_pairs(c_sb), c)
+            terms = (a_sb[q, half], c_sb) if a_first else (c_sb, a_sb[q, half])
+            nc.scalar.activation(into, transposed_sum(take("y%d%d" % (q, half), y_after), *terms), ACT.Tanh)
 
-        def make_y_in_pairs(q, half, into, pb, sbs):
+        def make_y_by_pairs(q, half, into, c_after, y_after):
             c_sb = passing([P, PACK, P], F32, "c_sb")
-            c = product(banks[pb], h_operand(q), wc_operand(half))
-            for u, sb in enumerate(sbs):
+            c = product(take("c%d%d" % (q, half), c_after)[:], h_operand(q), wc_operand(half), FIRST_PASS_FIRST)
+            for u in range(2):
                 nc.scalar.copy(by_pairs(c_sb)[:, u], c[:, u])
-            for u, sb in enumerate(sbs):
-                bank = banks[sb][:, 0:2 * P].rearrange("m (e j) -> m e j", e=2)
-                for term in (a_sb[q, half], c_sb):
-                    for e in range(2):
-                        nc.tensor.matmul(bank[:, e, :], lhsT=term[:, 2 * u + e, :], rhs=ident[:], is_transpose=True,
-                                         start=(term is not c_sb and e == 0), stop=(term is c_sb and e == 1))
-                nc.scalar.activation(into[:, 2 * u:2 * u + 2, :], bank, ACT.Tanh)
+            for u in range(2):
+                pair = slice(2 * u, 2 * u + 2)
+                bank = take("y%d%d_%d" % (q, half, u), y_after[u])
+                total = transposed_sum(bank, a_sb[q, half][:, pair, :], c_sb[:, pair, :])
+                nc.scalar.activation(into[:, pair, :], total, ACT.Tanh)
 
-        pages = [held([P, T2], F32, "page%d" % t) for t in range(HALVES * PACK)]
-        for t, page in enumerate(pages):
-            (nc.vector if t < 2 else nc.gpsimd).memset(page[:].bitcast(I32), 0)
+        pages = [held([P, T2], F32, "page%d" % n) for n in range(HALVES * PACK)]
+        for n, page in enumerate(pages):
+            (nc.vector if n < VECTOR_PAGES else nc.gpsimd).memset(page[:].bitcast(I32), 0)
 
-        def scatter(y, lo, hi, half):
-            rows = out[channels(half), :].rearrange("(m t) s -> m t s", t=PACK)
+        def scatter(y, q, half):
+            lo, hi = q * P, q * P + y.shape[2]
+            out_rows = out[channels(half), :].rearrange("(m t) s -> m t s", t=PACK)
             for t in range(PACK):
                 page = pages[half * PACK + t]
                 nc.vector.tensor_tensor(page[:].indirect(offs2_sb[:, lo // GROUP:hi // GROUP]),
                                         y[:, t, :], wgo_sb[:, lo:hi], ALU.mult)
                 if hi == S:
-                    nc.sync.dma_start(rows[:, t, :], page[:])
+                    nc.sync.dma_start(out_rows[:, t, :], page[:])
 
-        def y_tile(quarters, name):
-            return held([P, PACK, quarters * P], F32, name)
+        def y_tile(q, half, quarters=1):
+            return held([P, PACK, quarters * P], F32, "y%d%d" % (q, half))
 
-        for q, half, bank in ((0, 0, 0), (1, 0, 1), (0, 1, 2), (2, 0, 3), (1, 1, 4), (3, 0, 5)):
-            make_minus_b(q, half, banks[bank])
-        y = {}
-        for q, half in ((0, 0), (0, 1), (1, 0), (1, 1), (2, 0), (3, 0)):
-            y[q, half] = y_tile(1, "y%d%d" % (q, half))
-        make_a(0, 0, 3, True)
-        make_h(0, 0, 0, True)
-        make_a(1, 0, 4, True)
-        make_minus_b(2, 1, banks[6])
-        make_minus_b(3, 1, banks[7])
-        make_a_in_pieces(0, 1, (5, 6))
-        make_h(0, 1, 2, True)
-        make_a(2, 0, 3, True)
-        make_h(1, 0, 1, False)
-        make_y_in_pairs(0, 0, y[0, 0], 3, (4, 0))
-        scatter(y[0, 0], 0, P, 0)
-        make_h(2, 0, 6, False)
-        make_a(1, 1, 5, False)
-        make_h(1, 1, 2, False)
-        make_y(0, 1, y[0, 1][:], 7, 1, (0, 1))
-        scatter(y[0, 1], 0, P, 1)
-        make_a(2, 1, 3, False)
-        make_h_on_scalar(2, 1, 4)
-        make_y(1, 0, y[1, 0][:], 4, 6, (0, 1), True)
-        scatter(y[1, 0], P, 2 * P, 0)
-        make_a(3, 0, 7, True)
-        make_y(1, 1, y[1, 1][:], 4, 2)
-        scatter(y[1, 1], P, 2 * P, 1)
-        make_h_on_scalar(3, 0, 0)
-        make_a(3, 1, 3, False)
-        make_h_on_scalar(3, 1, 1)
-        make_y(2, 0, y[2, 0][:], 6, 1, (0, 1))
-        scatter(y[2, 0], 2 * P, 3 * P, 0)
-        last = y_tile(2, "y_last")
-        make_y(2, 1, last[:, :, entries(0)], 6, 2)
-        make_y(3, 0, y[3, 0][:], 1, 4, (0, 1), True)
-        scatter(y[3, 0], 3 * P, S, 0)
-        make_y(3, 1, last[:, :, entries(1)], 1, 0)
-        scatter(last, 2 * P, S, 1)
+        for q, half in ((0, 0), (1, 0), (0, 1), (2, 0), (1, 1), (3, 0)):
+            make_minus_b(q, half)
+        y00, y01, y10, y11, y30 = y_tile(0, 0), y_tile(0, 1), y_tile(1, 0), y_tile(1, 1), y_tile(3, 0)
+
+        make_a(0, 0, after="b20")
+        make_h(0, 0, after="b00", b_first=True, place=LAST_PIECE)
+        make_a(1, 0, after="b11")
+        make_minus_b(2, 1)
+        make_minus_b(3, 1)
+        make_a_by_pieces(0, 1, after=("b30", "b21"))
+        make_h(0, 1, after="b01", b_first=True, parts=2)
+        make_a(2, 0, after="a00")
+        make_h(1, 0, after="b10", place=LAST_PIECE + 1)
+
+        make_y_by_pairs(0, 0, y00, c_after="a20", y_after=("a10", "h00"))
+        make_h(2, 0, after="a01_1")
+        make_a(1, 1, after="b31")
+        make_h(1, 1, after="h01")
+        scatter(y00, 0, 0)
+        make_y(0, 1, y01[:], c_after="a01_0", y_after="h10", order=FIRST_PASS_FIRST)
+        scatter(y01, 0, 1)
+
+        make_a(2, 1, after="c00")
+        quantise_h(2, 1, scale_on_scalar(2, 1, after="y00_0"))
+        make_y(1, 0, y10[:], c_after="h21", y_after="h20", order=FIRST_PASS_FIRST, a_first=True)
+        scatter(y10, 1, 0)
+        make_a(3, 0, after="c01")
+        make_y(1, 1, y11[:], c_after="c10", y_after="h11")
+        scatter(y11, 1, 1)
+        quantise_h(3, 0, scale_on_scalar(3, 0, after="y00_1"))
+        make_a(3, 1, after="a21")
+        h31 = scale_on_scalar(3, 1, after="y01", place=LAST_ROWS)
+        y20 = placed([P, PACK, P], F32, "y20", LAST_ROWS)
+        make_y(2, 0, y20[:], c_after="y10", y_after="h31", order=FIRST_PASS_FIRST, place=LAST_CODES)
+        quantise_h(3, 1, h31, codes=placed([P, P], U32, "h_codes31", LAST_CODES))
+        scatter(y20, 2, 0)
+        make_y_by_pairs(3, 0, y30, c_after="c20", y_after=("c11", "a31"))
+        scatter(y30, 3, 0)
+        y21 = y_tile(2, 1, quarters=2)
+        make_y(2, 1, y21[:, :, entries(0)], c_after="y11", y_after="a11")
+        make_y(3, 1, y21[:, :, entries(1)], c_after="a30", y_after="h30")
+        scatter(y21, 2, 1)

@@ -31,12 +31,25 @@ BANKS = 8
 PIECE = 256
 DEPTH = 3
 WARM_UPS = 4
-VECTOR_PAGES = 2
+VECTOR_PAGES = 3
+QPARTS = 2
+HPARTS = 4
+ROWS = ((0, 1), (1, 4))
+QRUNS = {(0, 0): ((0, 512),), (1, 0): ((0, 128),), (1, 256): ((128, 384), (384, 512)), (0, 512): (), (0, 768): ((0, 256), (256, 512)), (1, 512): ((0, 128),), (1, 768): ((128, 256), (256, 384)), (1, 896): ((384, 512),)}
+B_ON_VECTOR = ()
+SCALAR_PIECE = (0, 512)
+RUN = {512: 256, 256: 128, 128: 128}
+EARLY = 0
 KIB = 1024
 
-LAST_PIECE = 0
-LAST_CODES = 2
-LAST_ROWS = 4
+LAST_PIECE = 2 * KIB
+A20 = 64
+H00 = A20 + 2 * KIB
+H10 = H00 + KIB
+H01 = 19 * KIB
+WINDOWS = 15 * KIB
+C0 = 13 * KIB
+LATE_ROWS = 7 * KIB
 
 FIRST_PASS_FIRST = (0, 1)
 LAST_PASS_FIRST = (1, 0)
@@ -58,7 +71,7 @@ def tile_list_gamelan_slots_kernel(tc, tab_words, tab_scales, offs, wa, wb_words
             return ring.tile(shape, dtype, name=name, align_bytes=64)
 
         def placed(shape, dtype, name, place):
-            return shared.tile(shape, dtype, name=name, align_bytes=64, offset=place * KIB)
+            return shared.tile(shape, dtype, name=name, align_bytes=64, offset=place)
 
         offs_sb = keep.tile([P, S // GROUP], U16, name="offs_sb")
         offs2_sb = keep.tile([P, S // GROUP], U16, name="offs2_sb")
@@ -66,7 +79,7 @@ def tile_list_gamelan_slots_kernel(tc, tab_words, tab_scales, offs, wa, wb_words
         wb_sb = held([P, PASSES, 2 * H], U8, "wb_sb")
         nc.sync.dma_start(wb_sb[:].bitcast(I32), wb_words.rearrange("g p c -> p g c").bitcast(I32))
 
-        scale_window = [held([P, T], U8, "scale_window%d" % g) for g in range(PASSES)]
+        scale_window = [placed([P, T], U8, "scale_window%d" % g, WINDOWS + g * T) for g in range(PASSES)]
         for g in range(PASSES):
             nc.vector.memset(scale_window[g][:].bitcast(I32), 0)
             nc.sync.dma_start(scale_window[g][0:P:BLOCK_PARTITIONS, :].bitcast(I32), tab_scales[g].bitcast(I32))
@@ -141,22 +154,29 @@ def tile_list_gamelan_slots_kernel(tc, tab_words, tab_scales, offs, wa, wb_words
             for g in range(PASSES):
                 wa_codes[g, half] = held([P, PASS], U32, "wa_codes%d%d" % (g, half))
                 wa_plane[g, half] = held([P, PASS], U8, "wa_plane%d%d" % (g, half))
+        def round_wa(copy, g, lo, first, end):
+            half, column = divmod(lo, PASS)
+            to = wa_grouped[g, half][:, column + first:column + end, :].rearrange("p (c e) i -> p c i e", e=LINE)
+            copy(to, wa_raw[g, lo][:, :, first:end].rearrange("p i (c e) -> p c i e", e=LINE))
+
+        def round_on_scalar(to, source):
+            nc.scalar.activation(to, source, ACT.Copy)
+
+        def quantise_wa(g, half, first, end):
+            nc.vector.quantize_mx(out=wa_codes[g, half][:, first:end].bitcast(FP8X4),
+                                  scales=wa_plane[g, half][:, first:end],
+                                  in_=wa_grouped[g, half][:, first:end, :].rearrange("p c i -> p (c i)"))
+
         for g, lo, width in wa_pieces:
             half, column = divmod(lo, PASS)
             if column == 0:
                 wa_grouped[g, half] = held([P, PASS, PACK], BF16, "wa_grouped%d%d" % (g, half))
-            to = wa_grouped[g, half][:, column:column + width, :].rearrange("p (c e) i -> p c i e", e=LINE)
-            source = wa_raw[g, lo][:].rearrange("p i (c e) -> p c i e", e=LINE)
-            if width > PIECE:
-                share = (width - PIECE) // LINE
-                nc.scalar.activation(to[:, 0:share], source[:, 0:share], ACT.Copy)
-                to, source = to[:, share:], source[:, share:]
-            nc.vector.tensor_copy(to, source)
-            if half == HALVES - 1 or column + width == PASS:
-                columns = slice(column if half == HALVES - 1 else 0, column + width)
-                nc.vector.quantize_mx(out=wa_codes[g, half][:, columns].bitcast(FP8X4),
-                                      scales=wa_plane[g, half][:, columns],
-                                      in_=wa_grouped[g, half][:, columns, :].rearrange("p c i -> p (c i)"))
+            on_scalar = (g, lo) == SCALAR_PIECE
+            run = width if on_scalar else RUN[width]
+            for first in range(0, width, run):
+                round_wa(round_on_scalar if on_scalar else nc.vector.tensor_copy, g, lo, first, first + run)
+            for first, end in QRUNS[g, lo]:
+                quantise_wa(g, half, first, end)
 
         h_codes, h_plane = {}, {}
 
@@ -220,44 +240,56 @@ def tile_list_gamelan_slots_kernel(tc, tab_words, tab_scales, offs, wa, wb_words
             bank_of["b%d%d" % (q, half)] = bank
             minus_b[q, half] = held([P, PACK, P], F32, "minus_b%d%d" % (q, half))
             b = product(bank[:], v_operand(q), wb_operand(half), FIRST_PASS_FIRST)
-            nc.scalar.activation(by_pairs(minus_b[q, half]), b, ACT.Copy, scale=-1.0)
+            if len(minus_b) in B_ON_VECTOR:
+                nc.vector.tensor_scalar(by_pairs(minus_b[q, half]), b, -1.0, None, ALU.mult)
+            else:
+                nc.scalar.activation(by_pairs(minus_b[q, half]), b, ACT.Copy, scale=-1.0)
 
-        def make_a(q, half, after):
-            a_sb[q, half] = held([P, PACK, P], F32, "a_sb%d%d" % (q, half))
-            order = FIRST_PASS_FIRST if half == 0 else LAST_PASS_FIRST
-            a = product(take("a%d%d" % (q, half), after)[:], v_operand(q), wa_operand(half), order)
-            nc.scalar.copy(by_pairs(a_sb[q, half]), a)
-
-        def make_a_by_pieces(q, half, after):
-            a_sb[q, half] = held([P, PACK, P], F32, "a_sb%d%d" % (q, half))
-            for n in range(PASS // PIECE):
-                bank = take("a%d%d_%d" % (q, half, n), after[n])
-                a = product(bank[:, 0:PIECE], v_operand(q), wa_operand(half, slice(n * PIECE, (n + 1) * PIECE)),
-                            FIRST_PASS_FIRST)
-                nc.scalar.copy(by_pairs(a_sb[q, half])[:, :, n * PIECE // PACK:(n + 1) * PIECE // PACK, :], a)
+        def make_a(q, half, after, steps=((0, 0, PASS), (1, 0, PASS)), copy=nc.scalar.copy, place=None):
+            if (q, half) not in a_sb:
+                name = "a_sb%d%d" % (q, half)
+                a_sb[q, half] = held([P, PACK, P], F32, name) if place is None \
+                    else placed([P, PACK, P], F32, name, place)
+            lo, hi = min(step[1] for step in steps), max(step[2] for step in steps)
+            bank = take("a%d%d%s" % (q, half, "_%d" % lo if lo else ""), after)
+            for g, first, end in steps:
+                lhs, lhs_scale = v_operand(q)(g)
+                rhs, rhs_scale = wa_operand(half, slice(first, end))(g)
+                nc.tensor.matmul_mx(out=bank[:, first - lo:end - lo], lhsT=lhs, lhsT_scale=lhs_scale, rhs=rhs,
+                                    rhs_scale=rhs_scale, start=((g, first, end) == steps[0]),
+                                    stop=((g, first, end) == steps[-1]))
+            a = bank[:, 0:hi - lo].rearrange("p (m u e) -> p u m e", u=2, e=2)
+            copy(by_pairs(a_sb[q, half])[:, :, lo // PACK:hi // PACK, :], a)
 
         def difference(q, half, after, b_first):
             terms = (minus_b[q, half], a_sb[q, half]) if b_first else (a_sb[q, half], minus_b[q, half])
             return transposed_sum(take("h%d%d" % (q, half), after), *terms)
 
-        def quantise_h(q, half, h, codes=None):
-            h_codes[q, half] = held([P, P], U32, "h_codes%d%d" % (q, half)) if codes is None else codes
+        def quantise_h(q, half, h, parts=1):
+            h_codes[q, half] = held([P, P], U32, "h_codes%d%d" % (q, half))
             h_plane[q, half] = held([P, P], U8, "h_plane%d%d" % (q, half))
-            nc.vector.quantize_mx(out=h_codes[q, half][:].bitcast(FP8X4), scales=h_plane[q, half][:],
-                                  in_=h[:].rearrange("m j t -> m (j t)"))
+            for lo in range(0, P, P // parts):
+                run = slice(lo, lo + P // parts)
+                nc.vector.quantize_mx(out=h_codes[q, half][:, run].bitcast(FP8X4), scales=h_plane[q, half][:, run],
+                                      in_=h[:, run, :].rearrange("m j t -> m (j t)"))
 
-        def make_h(q, half, after, b_first=False, parts=1, place=None):
-            total = difference(q, half, after, b_first).rearrange("m t j -> m j t")
-            size = passing([P, P, PACK], F32, "size")
-            runs = [slice(lo, lo + P // parts) for lo in range(0, P, P // parts)]
-            for run in runs:
-                nc.scalar.activation(size[:, run, :], total[:, run, :], ACT.Abs)
+        sizes = {}
+
+        def make_size(q, half, after, parts=1):
+            total = difference(q, half, after, True).rearrange("m t j -> m j t")
+            sizes[q, half] = held([P, P, PACK], F32, "size%d%d" % (q, half))
+            for lo in range(0, P, P // parts):
+                run = slice(lo, lo + P // parts)
+                nc.scalar.activation(sizes[q, half][:, run, :], total[:, run, :], ACT.Abs)
+
+        def scale_on_vector(q, half, parts=1, place=None):
             h = passing([P, P, PACK], BF16, "h") if place is None \
                 else placed([P, P, PACK], BF16, "h%d%d" % (q, half), place)
             factor = sens_sb[:, half:half + 1, :].to_broadcast([P, P // parts, PACK])
-            for run in runs:
-                nc.vector.tensor_tensor(h[:, run, :], size[:, run, :], factor, ALU.mult)
-            quantise_h(q, half, h)
+            for lo in range(0, P, P // parts):
+                run = slice(lo, lo + P // parts)
+                nc.vector.tensor_tensor(h[:, run, :], sizes[q, half][:, run, :], factor, ALU.mult)
+            quantise_h(q, half, h, min(parts, QPARTS))
 
         def scale_on_scalar(q, half, after, place=None):
             total = difference(q, half, after, False)
@@ -277,75 +309,95 @@ def tile_list_gamelan_slots_kernel(tc, tab_words, tab_scales, offs, wa, wb_words
             c = product(take("c%d%d" % (q, half), c_after)[:], h_operand(q), wc_operand(half), order)
             nc.scalar.copy(by_pairs(c_sb), c)
             terms = (a_sb[q, half], c_sb) if a_first else (c_sb, a_sb[q, half])
-            nc.scalar.activation(into, transposed_sum(take("y%d%d" % (q, half), y_after), *terms), ACT.Tanh)
+            total = transposed_sum(take("y%d%d" % (q, half), y_after), *terms)
+            lo = 0
+            for part in into:
+                nc.scalar.activation(part, total[:, lo:lo + part.shape[1], :], ACT.Tanh)
+                lo = lo + part.shape[1]
 
-        def make_y_by_pairs(q, half, into, c_after, y_after):
-            c_sb = passing([P, PACK, P], F32, "c_sb")
-            c = product(take("c%d%d" % (q, half), c_after)[:], h_operand(q), wc_operand(half), FIRST_PASS_FIRST)
-            for u in range(2):
-                nc.scalar.copy(by_pairs(c_sb)[:, u], c[:, u])
-            for u in range(2):
-                pair = slice(2 * u, 2 * u + 2)
+        def make_y_by_pairs(q, half, into, c_after, y_after, a_first=(True, True), rows=((0, 2), (2, 4)), place=None):
+            c_sb = passing([P, PACK, P], F32, "c_sb") if place is None \
+                else placed([P, PACK, P], F32, "c_sb%d%d" % (q, half), place)
+            bank = take("c%d%d" % (q, half), c_after)
+            product(bank[:], h_operand(q), wc_operand(half), FIRST_PASS_FIRST)
+            c = bank[:].rearrange("p (m t) -> p t m", t=PACK)
+            for lo, hi in rows:
+                nc.scalar.copy(c_sb[:, lo:hi, :], c[:, lo:hi, :])
+            for u, (lo, hi) in enumerate(rows):
                 bank = take("y%d%d_%d" % (q, half, u), y_after[u])
-                total = transposed_sum(bank, a_sb[q, half][:, pair, :], c_sb[:, pair, :])
-                nc.scalar.activation(into[:, pair, :], total, ACT.Tanh)
+                terms = (a_sb[q, half][:, lo:hi, :], c_sb[:, lo:hi, :])
+                total = transposed_sum(bank, *(terms if a_first[u] else terms[::-1]))
+                nc.scalar.activation(into[:, lo:hi, :], total, ACT.Tanh)
 
-        pages = [held([P, T2], F32, "page%d" % n) for n in range(HALVES * PACK)]
+        pages = [placed([P, T2], F32, "page%d" % n, WINDOWS) if n == VECTOR_PAGES - 1
+                 else held([P, T2], F32, "page%d" % n) for n in range(HALVES * PACK)]
         for n, page in enumerate(pages):
             (nc.vector if n < VECTOR_PAGES else nc.gpsimd).memset(page[:].bitcast(I32), 0)
 
-        def scatter(y, q, half):
+        def scatter(y, q, half, rows=range(PACK)):
             lo, hi = q * P, q * P + y.shape[2]
             out_rows = out[channels(half), :].rearrange("(m t) s -> m t s", t=PACK)
-            for t in range(PACK):
+            for n, t in enumerate(rows):
                 page = pages[half * PACK + t]
                 nc.vector.tensor_tensor(page[:].indirect(offs2_sb[:, lo // GROUP:hi // GROUP]),
-                                        y[:, t, :], wgo_sb[:, lo:hi], ALU.mult)
+                                        y[:, n, :], wgo_sb[:, lo:hi], ALU.mult)
                 if hi == S:
                     nc.sync.dma_start(out_rows[:, t, :], page[:])
 
         def y_tile(q, half, quarters=1):
             return held([P, PACK, quarters * P], F32, "y%d%d" % (q, half))
 
-        for q, half in ((0, 0), (1, 0), (0, 1), (2, 0), (1, 1), (3, 0)):
+        for q, half in ((0, 0), (1, 0), (3, 0), (2, 1), (0, 1), (1, 1), (2, 0), (3, 1)):
             make_minus_b(q, half)
-        y00, y01, y10, y11, y30 = y_tile(0, 0), y_tile(0, 1), y_tile(1, 0), y_tile(1, 1), y_tile(3, 0)
+        y00, y01, y30 = y_tile(0, 0), y_tile(0, 1), y_tile(3, 0)
+        last = PASS - PIECE // 2
+        by_pieces = ((0, 0, PASS), (1, 0, PIECE), (1, PIECE, PASS))
 
-        make_a(0, 0, after="b20")
-        make_h(0, 0, after="b00", b_first=True, place=LAST_PIECE)
-        make_a(1, 0, after="b11")
-        make_minus_b(2, 1)
-        make_minus_b(3, 1)
-        make_a_by_pieces(0, 1, after=("b30", "b21"))
-        make_h(0, 1, after="b01", b_first=True, parts=2)
-        make_a(2, 0, after="a00")
-        make_h(1, 0, after="b10", place=LAST_PIECE + 1)
-
-        make_y_by_pairs(0, 0, y00, c_after="a20", y_after=("a10", "h00"))
-        make_h(2, 0, after="a01_1")
-        make_a(1, 1, after="b31")
-        make_h(1, 1, after="h01")
+        make_a(0, 0, after="b30")
+        make_size(0, 0, after="b00")
+        scale_on_vector(0, 0, place=H00)
+        make_a(1, 0, after="b21")
+        make_size(1, 0, after="b10")
+        make_a(0, 1, after="b31", steps=((0, 0, PIECE), (0, PIECE, last), (1, 0, PIECE), (1, PIECE, last)))
+        make_a(0, 1, after="h00", steps=((0, last, PASS), (1, last, PASS)))
+        make_size(0, 1, after="b01", parts=HPARTS)
+        scale_on_vector(0, 1, parts=HPARTS, place=H01)
+        make_a(1, 1, after="a10", steps=by_pieces)
+        make_a(2, 0, after="a00", copy=nc.vector.tensor_copy, place=A20)
+        scale_on_vector(1, 0, place=H10)
+        make_size(2, 0, after="b20")
+        make_size(1, 1, after="b11")
+        make_y_by_pairs(0, 0, y00, c_after="a01", y_after=("a01_384", "a20"), rows=ROWS, place=C0)
+        scale_on_vector(2, 0)
+        scale_on_vector(1, 1)
+        make_a(2, 1, after="h10", steps=((1, 0, PASS), (0, 0, PASS)), copy=nc.vector.tensor_copy, place=H01)
+        make_a(3, 0, after="h01")
         scatter(y00, 0, 0)
-        make_y(0, 1, y01[:], c_after="a01_0", y_after="h10", order=FIRST_PASS_FIRST)
+        make_y(0, 1, [y01[:]], c_after="a11", y_after="y00_0", a_first=True, order=FIRST_PASS_FIRST, place=C0)
         scatter(y01, 0, 1)
 
-        make_a(2, 1, after="c00")
-        quantise_h(2, 1, scale_on_scalar(2, 1, after="y00_0"))
-        make_y(1, 0, y10[:], c_after="h21", y_after="h20", order=FIRST_PASS_FIRST, a_first=True)
-        scatter(y10, 1, 0)
-        make_a(3, 0, after="c01")
-        make_y(1, 1, y11[:], c_after="c10", y_after="h11")
-        scatter(y11, 1, 1)
-        quantise_h(3, 0, scale_on_scalar(3, 0, after="y00_1"))
-        make_a(3, 1, after="a21")
-        h31 = scale_on_scalar(3, 1, after="y01", place=LAST_ROWS)
-        y20 = placed([P, PACK, P], F32, "y20", LAST_ROWS)
-        make_y(2, 0, y20[:], c_after="y10", y_after="h31", order=FIRST_PASS_FIRST, place=LAST_CODES)
-        quantise_h(3, 1, h31, codes=placed([P, P], U32, "h_codes31", LAST_CODES))
+        def late(q, half, after, n, y_name, rows=PACK):
+            place = LATE_ROWS + n * 2 * KIB
+            quantise_h(q, half, scale_on_scalar(q, half, after=after, place=place))
+            return placed([P, rows, P], F32, y_name, place)
+
+        y10 = late(2, 1, "c00", 0, "y10", PACK - 1)
+        y10_first = held([P, 1, P], F32, "y10_first")
+        make_y(1, 0, [y10_first[:], y10[:]], c_after="y00_1", y_after="y01", order=FIRST_PASS_FIRST, a_first=True)
+        scatter(y10_first, 1, 0, range(1))
+        scatter(y10, 1, 0, range(1, PACK))
+        y11 = late(3, 0, "h21", 1, "y11", PACK - 1)
+        y11_first = held([P, 1, P], F32, "y11_first")
+        make_y(1, 1, [y11_first[:], y11[:]], c_after="c10", y_after="h11")
+        scatter(y11_first, 1, 1, range(1))
+        scatter(y11, 1, 1, range(1, PACK))
+        make_a(3, 1, after="c01")
+        y20 = late(3, 1, "h30", 2, "y20")
+        make_y(2, 0, [y20[:]], c_after="y10", y_after="a31", order=FIRST_PASS_FIRST, a_first=True)
         scatter(y20, 2, 0)
-        make_y_by_pairs(3, 0, y30, c_after="c20", y_after=("c11", "a31"))
+        make_y_by_pairs(3, 0, y30, c_after="h31", y_after=("y11", "c11"))
         scatter(y30, 3, 0)
         y21 = y_tile(2, 1, quarters=2)
-        make_y(2, 1, y21[:, :, entries(0)], c_after="y11", y_after="a11")
-        make_y(3, 1, y21[:, :, entries(1)], c_after="a30", y_after="h30")
+        make_y(2, 1, [y21[:, :, entries(0)]], c_after="c20", y_after="h20")
+        make_y(3, 1, [y21[:, :, entries(1)]], c_after="y20", y_after="a30")
         scatter(y21, 2, 1)

@@ -214,10 +214,10 @@ def tile_list_gamelan_slots_kernel(tc, tab_words, tab_scales, offs, wa, wb_words
                 (lhs, lhs_scale), (rhs, rhs_scale) = stationary(g), moving(g)
                 nc.tensor.matmul_mx(out=into, lhsT=lhs, lhsT_scale=lhs_scale, rhs=rhs, rhs_scale=rhs_scale,
                                     start=(g == order[0]), stop=(g == order[-1]))
-            return into.rearrange("p (m u e) -> p u m e", u=2, e=2)
+            return into.rearrange("p (m t) -> p t m", t=PACK)
 
         def by_pairs(tile):
-            return tile[:].rearrange("p (u e) m -> p u m e", e=2)
+            return tile[:]
 
         def transposed_sum(bank, first, second):
             count = first.shape[1]
@@ -258,8 +258,8 @@ def tile_list_gamelan_slots_kernel(tc, tab_words, tab_scales, offs, wa, wb_words
                 nc.tensor.matmul_mx(out=bank[:, first - lo:end - lo], lhsT=lhs, lhsT_scale=lhs_scale, rhs=rhs,
                                     rhs_scale=rhs_scale, start=((g, first, end) == steps[0]),
                                     stop=((g, first, end) == steps[-1]))
-            a = bank[:, 0:hi - lo].rearrange("p (m u e) -> p u m e", u=2, e=2)
-            copy(by_pairs(a_sb[q, half])[:, :, lo // PACK:hi // PACK, :], a)
+            a = bank[:, 0:hi - lo].rearrange("p (m t) -> p t m", t=PACK)
+            copy(a_sb[q, half][:, :, lo // PACK:hi // PACK], a)
 
         def difference(q, half, after, b_first):
             terms = (minus_b[q, half], a_sb[q, half]) if b_first else (a_sb[q, half], minus_b[q, half])

@@ -31,14 +31,14 @@ BANKS = 8
 PIECE = 256
 DEPTH = 3
 WARM_UPS = 4
-VECTOR_PAGES = 3
-QPARTS = 2
-HPARTS = 4
+VECTOR_PAGES = 2
+QPARTS = 1
+HPARTS = 2
 ROWS = ((0, 1), (1, 4))
-QRUNS = {(0, 0): ((0, 512),), (1, 0): ((0, 128),), (1, 256): ((128, 384), (384, 512)), (0, 512): (), (0, 768): ((0, 256), (256, 512)), (1, 512): ((0, 128),), (1, 768): ((128, 256), (256, 384)), (1, 896): ((384, 512),)}
+QRUNS = {(0, 0): ((0, 512),), (1, 0): (), (1, 256): ((0, 512),), (0, 512): ((0, 256),), (0, 768): ((256, 512),), (1, 512): ((0, 256),), (1, 768): ((256, 384),), (1, 896): ((384, 512),)}
 B_ON_VECTOR = ()
 SCALAR_PIECE = (0, 512)
-RUN = {512: 256, 256: 128, 128: 128}
+RUN = {512: 256, 256: 256, 128: 128}
 EARLY = 0
 KIB = 1024
 
@@ -329,8 +329,7 @@ def tile_list_gamelan_slots_kernel(tc, tab_words, tab_scales, offs, wa, wb_words
                 total = transposed_sum(bank, *(terms if a_first[u] else terms[::-1]))
                 nc.scalar.activation(into[:, lo:hi, :], total, ACT.Tanh)
 
-        pages = [placed([P, T2], F32, "page%d" % n, WINDOWS) if n == VECTOR_PAGES - 1
-                 else held([P, T2], F32, "page%d" % n) for n in range(HALVES * PACK)]
+        pages = [held([P, T2], F32, "page%d" % n) for n in range(HALVES * PACK)]
         for n, page in enumerate(pages):
             (nc.vector if n < VECTOR_PAGES else nc.gpsimd).memset(page[:].bitcast(I32), 0)
 

@@ -73,6 +73,11 @@ def tile_list_gamelan_slots_kernel(tc, tab_words, tab_scales, offs, wa, wb_words
         def placed(shape, dtype, name, place):
             return shared.tile(shape, dtype, name=name, align_bytes=64, offset=place)
 
+        def clear_on_vector(words):
+            cut = words.shape[1] // 2 + 1
+            nc.vector.memset(words[:, 0:cut], 0)
+            nc.vector.memset(words[:, cut:], 0)
+
         offs_sb = keep.tile([P, S // GROUP], U16, name="offs_sb")
         offs2_sb = keep.tile([P, S // GROUP], U16, name="offs2_sb")
         nc.sync.dma_start(offs_sb[:], offs)
@@ -81,13 +86,16 @@ def tile_list_gamelan_slots_kernel(tc, tab_words, tab_scales, offs, wa, wb_words
 
         scale_window = [placed([P, T], U8, "scale_window%d" % g, WINDOWS + g * T) for g in range(PASSES)]
         for g in range(PASSES):
-            nc.vector.memset(scale_window[g][:].bitcast(I32), 0)
+            if g == 0:
+                nc.gpsimd.memset(scale_window[g][:].bitcast(I32), 0)
+            else:
+                clear_on_vector(scale_window[g][:].bitcast(I32))
             nc.sync.dma_start(scale_window[g][0:P:BLOCK_PARTITIONS, :].bitcast(I32), tab_scales[g].bitcast(I32))
 
         v_plane = held([P, PASSES, S], U8, "v_plane")
         wb_plane = held([P, PASSES, H], U8, "wb_plane")
-        nc.vector.memset(v_plane[:].bitcast(I32), 0)
-        nc.gpsimd.memset(wb_plane[:].bitcast(I32), 0)
+        clear_on_vector(v_plane[:].rearrange("p g j -> p (g j)").bitcast(I32))
+        clear_on_vector(wb_plane[:].rearrange("p g j -> p (g j)").bitcast(I32))
 
         def load_plane(plane, scales):
             for r in range(SCALE_ROWS):
@@ -97,7 +105,7 @@ def tile_list_gamelan_slots_kernel(tc, tab_words, tab_scales, offs, wa, wb_words
         ident = held([P, P], F32, "ident")
         make_identity(nc, ident[:])
         sens_sb = held([P, HALVES, PACK], F32, "sens_sb")
-        nc.gpsimd.dma_start(sens_sb[:], sens.rearrange("(half m t) -> m half t", half=HALVES, t=PACK))
+        nc.scalar.dma_start(sens_sb[:], sens.rearrange("(half m t) -> m half t", half=HALVES, t=PACK))
 
         word_window = [held([P, T], I32, "word_window%d" % g) for g in range(PASSES)]
 
@@ -139,6 +147,13 @@ def tile_list_gamelan_slots_kernel(tc, tab_words, tab_scales, offs, wa, wb_words
         def load_wc(half):
             words = wc_words.rearrange("g p c i -> p g (c i)")[:, :, half * PASS * PACK:(half + 1) * PASS * PACK]
             nc.sync.dma_start(wc_sb[half][:], words.bitcast(I32))
+
+        pages = [held([P, T2], F32, "page%d" % n) for n in range(HALVES * PACK)]
+        for n, page in enumerate(pages):
+            if n < VECTOR_PAGES:
+                clear_on_vector(page[:].bitcast(I32))
+            else:
+                nc.gpsimd.memset(page[:].bitcast(I32), 0)
 
         load_wc(0)
         wc_plane = held([P, PASSES, H], U8, "wc_plane")
@@ -329,9 +344,6 @@ def tile_list_gamelan_slots_kernel(tc, tab_words, tab_scales, offs, wa, wb_words
                 total = transposed_sum(bank, *(terms if a_first[u] else terms[::-1]))
                 nc.scalar.activation(into[:, lo:hi, :], total, ACT.Tanh)
 
-        pages = [held([P, T2], F32, "page%d" % n) for n in range(HALVES * PACK)]
-        for n, page in enumerate(pages):
-            (nc.vector if n < VECTOR_PAGES else nc.gpsimd).memset(page[:].bitcast(I32), 0)
 
         def scatter(y, q, half, rows=range(PACK)):
             lo, hi = q * P, q * P + y.shape[2]

@@ -32,7 +32,7 @@ PIECE = 256
 DEPTH = 3
 WARM_UPS = 4
 VECTOR_PAGES = 2
-QPARTS = 1
+QPARTS = 2
 HPARTS = 2
 ROWS = ((0, 1), (1, 4))
 QRUNS = {(0, 0): ((0, 512),), (1, 0): (), (1, 256): ((0, 512),), (0, 512): ((0, 256),), (0, 768): ((256, 512),), (1, 512): ((0, 256),), (1, 768): ((256, 384),), (1, 896): ((384, 512),)}
@@ -105,7 +105,6 @@ def tile_list_gamelan_slots_kernel(tc, tab_words, tab_scales, offs, wa, wb_words
         ident = held([P, P], F32, "ident")
         make_identity(nc, ident[:])
         sens_sb = held([P, HALVES, PACK], F32, "sens_sb")
-        nc.scalar.dma_start(sens_sb[:], sens.rearrange("(half m t) -> m half t", half=HALVES, t=PACK))
 
         word_window = [held([P, T], I32, "word_window%d" % g) for g in range(PASSES)]
 
@@ -142,6 +141,7 @@ def tile_list_gamelan_slots_kernel(tc, tab_words, tab_scales, offs, wa, wb_words
             piece = wa[g * PASS:(g + 1) * PASS, lo:lo + width]
             nc.sync.dma_start(wa_raw[g, lo][:], piece.rearrange("(p i) c -> p i c", i=PACK))
 
+        nc.sync.dma_start(sens_sb[:], sens.rearrange("(half m t) -> m half t", half=HALVES, t=PACK))
         wc_sb = [held([P, PASSES, PASS], I32, "wc_sb%d" % half) for half in range(HALVES)]
 
         def load_wc(half):
@@ -315,7 +315,8 @@ def tile_list_gamelan_slots_kernel(tc, tab_words, tab_scales, offs, wa, wb_words
             for t in range(PACK):
                 nc.scalar.activation(h_rows[:, t, :], size[:, t, :], ACT.Copy, scale=sens_sb[:, half, t:t + 1])
             h = passing([P, P, PACK], BF16, "h")
-            nc.scalar.copy(h[:], h_rows[:].rearrange("m t j -> m j t"))
+            nc.scalar.copy(h[:].rearrange("m (c e) t -> m c t e", e=LINE),
+                           h_rows[:].rearrange("m t (c e) -> m c t e", e=LINE))
             return h
 
         def make_y(q, half, into, c_after, y_after, order=LAST_PASS_FIRST, a_first=False, place=None):

@@ -80,9 +80,9 @@ def tile_list_gamelan_slots_kernel(tc, tab_words, tab_scales, offs, wa, wb_words
 
         offs_sb = keep.tile([P, S // GROUP], U16, name="offs_sb")
         offs2_sb = keep.tile([P, S // GROUP], U16, name="offs2_sb")
-        nc.sync.dma_start(offs_sb[:], offs)
         wb_sb = held([P, PASSES, 2 * H], U8, "wb_sb")
         nc.sync.dma_start(wb_sb[:].bitcast(I32), wb_words.rearrange("g p c -> p g c").bitcast(I32))
+        nc.sync.dma_start(offs_sb[:], offs)
 
         scale_window = [placed([P, T], U8, "scale_window%d" % g, WINDOWS + g * T) for g in range(PASSES)]
         for g in range(PASSES):
@@ -90,7 +90,7 @@ def tile_list_gamelan_slots_kernel(tc, tab_words, tab_scales, offs, wa, wb_words
                 nc.gpsimd.memset(scale_window[g][:].bitcast(I32), 0)
             else:
                 clear_on_vector(scale_window[g][:].bitcast(I32))
-            nc.sync.dma_start(scale_window[g][0:P:BLOCK_PARTITIONS, :].bitcast(I32), tab_scales[g].bitcast(I32))
+            nc.sync.dma_start(scale_window[g][SCALE_ROWS:P:BLOCK_PARTITIONS, :].bitcast(I32), tab_scales[g].bitcast(I32))
 
         v_plane = held([P, PASSES, S], U8, "v_plane")
         wb_plane = held([P, PASSES, H], U8, "wb_plane")
@@ -120,7 +120,7 @@ def tile_list_gamelan_slots_kernel(tc, tab_words, tab_scales, offs, wa, wb_words
             nc.vector.tensor_copy(v_scale[:, g, :], scale_window[g][:].indirect(offs_sb[:]))
         for r in range(SCALE_ROWS):
             nc.sync.dma_start(v_plane[r:P:QUADRANT].rearrange("p g j -> p (g j)").bitcast(I32),
-                              v_scale[BLOCK_PARTITIONS * r:P:QUADRANT].rearrange("p g j -> p (g j)").bitcast(I32))
+                              v_scale[BLOCK_PARTITIONS * r + SCALE_ROWS:P:QUADRANT].rearrange("p g j -> p (g j)").bitcast(I32))
 
         v_codes = [held([P, S], U32, "v_codes%d" % g) for g in range(PASSES)]
         for g in range(PASSES):

from contextlib import ExitStack

import concourse.mybir as mybir
from concourse.masks import make_identity

K, H, T, S, T2 = 1024, 1024, 2048, 512, 1024
FLOPS = 3 * 2 * K * H * S

F32 = mybir.dt.float32
BF16 = mybir.dt.bfloat16
I32 = mybir.dt.int32
U32 = mybir.dt.uint32
U16 = mybir.dt.uint16
U8 = mybir.dt.uint8
FP8X4 = mybir.dt.float8_e4m3fn_x4
FP4X4 = mybir.dt.float4_e2m1fn_x4
ACT = mybir.ActivationFunctionType
ALU = mybir.AluOpType

P = 128
PACK = 4
PASS = P * PACK
PASSES = K // PASS
HALVES = H // PASS
QUADRANT = 32
SCALE_ROWS = 4
BLOCK_PARTITIONS = 8
GROUP = 16
LINE = 4
BANKS = 8
PIECE = 256
DEPTH = 3
WARM_UPS = 4
VECTOR_PAGES = 2
QPARTS = 2
HPARTS = 2
ROWS = ((0, 1), (1, 4))
QRUNS = {(0, 0): ((0, 512),), (1, 0): (), (1, 256): ((0, 512),), (0, 512): ((0, 256),), (0, 768): ((256, 512),), (1, 512): ((0, 256),), (1, 768): ((256, 384),), (1, 896): ((384, 512),)}
B_ON_VECTOR = ()
SCALAR_PIECE = (0, 512)
RUN = {512: 256, 256: 256, 128: 128}
EARLY = 0
KIB = 1024

LAST_PIECE = 2 * KIB
A20 = 64
H00 = A20 + 2 * KIB
H10 = H00 + KIB
H01 = 19 * KIB
WINDOWS = 15 * KIB
C0 = 13 * KIB
LATE_ROWS = 7 * KIB

FIRST_PASS_FIRST = (0, 1)
LAST_PASS_FIRST = (1, 0)


def tile_list_gamelan_slots_kernel(tc, tab_words, tab_scales, offs, wa, wb_words, wb_scales, sens,
                                                wc_words, wc_scales, wgo, offs2, out):
    nc = tc.nc
    with ExitStack() as ctx:
        keep = ctx.enter_context(tc.tile_pool(name="keep", bufs=1))
        ring = ctx.enter_context(tc.tile_pool(name="ring", bufs=DEPTH))
        shared = ctx.enter_context(tc.tile_pool(name="shared", bufs=1))
        psum = ctx.enter_context(tc.psum_pool(name="psum", bufs=1))

        def held(shape, dtype, name):
            return keep.tile(shape, dtype, name=name, align_bytes=64)

        def passing(shape, dtype, name):
            return ring.tile(shape, dtype, name=name, align_bytes=64)

        def placed(shape, dtype, name, place):
            return shared.tile(shape, dtype, name=name, align_bytes=64, offset=place)

        def clear_on_vector(words):
            cut = words.shape[1] // 2 + 1
            nc.vector.memset(words[:, 0:cut], 0)
            nc.vector.memset(words[:, cut:], 0)

        offs_sb = keep.tile([P, S // GROUP], U16, name="offs_sb")
        offs2_sb = keep.tile([P, S // GROUP], U16, name="offs2_sb")
        wb_sb = held([P, PASSES, 2 * H], U8, "wb_sb")
        nc.sync.dma_start(wb_sb[:].bitcast(I32), wb_words.rearrange("g p c -> p g c").bitcast(I32))
        nc.sync.dma_start(offs_sb[:], offs)

        scale_window = [placed([P, T], U8, "scale_window%d" % g, WINDOWS + g * T) for g in range(PASSES)]
        for g in range(PASSES):
            if g == 0:
                nc.gpsimd.memset(scale_window[g][:].bitcast(I32), 0)
            else:
                clear_on_vector(scale_window[g][:].bitcast(I32))
            nc.sync.dma_start(scale_window[g][SCALE_ROWS:P:BLOCK_PARTITIONS, :].bitcast(I32), tab_scales[g].bitcast(I32))

        v_plane = held([P, PASSES, S], U8, "v_plane")
        wb_plane = held([P, PASSES, H], U8, "wb_plane")
        clear_on_vector(v_plane[:].rearrange("p g j -> p (g j)").bitcast(I32))
        clear_on_vector(wb_plane[:].rearrange("p g j -> p (g j)").bitcast(I32))

        def load_plane(plane, scales):
            for r in range(SCALE_ROWS):
                nc.sync.dma_start(plane[r:P:QUADRANT].bitcast(I32),
                                  scales[:, r::SCALE_ROWS, :].rearrange("g d c -> d g c").bitcast(I32))

        ident = held([P, P], F32, "ident")
        make_identity(nc, ident[:])
        sens_sb = held([P, HALVES, PACK], F32, "sens_sb")

        word_window = [held([P, T], I32, "word_window%d" % g) for g in range(PASSES)]

        def load_words(g):
            nc.sync.dma_start(word_window[g][:], tab_words[g].rearrange("p t i -> p (t i)").bitcast(I32))

        load_words(0)
        load_plane(wb_plane, wb_scales)
        load_words(1)

        v_scale = held([P, PASSES, S], U8, "v_scale")
        for g in range(PASSES):
            nc.vector.tensor_copy(v_scale[:, g, :], scale_window[g][:].indirect(offs_sb[:]))
        for r in range(SCALE_ROWS):
            nc.sync.dma_start(v_plane[r:P:QUADRANT].rearrange("p g j -> p (g j)").bitcast(I32),
                              v_scale[BLOCK_PARTITIONS * r + SCALE_ROWS:P:QUADRANT].rearrange("p g j -> p (g j)").bitcast(I32))

        v_codes = [held([P, S], U32, "v_codes%d" % g) for g in range(PASSES)]
        for g in range(PASSES):
            length = S // 2 if g == PASSES - 1 else S
            for lo in range(0, S, length):
                nc.vector.tensor_copy(v_codes[g][:, lo:lo + length], word_window[g][:].bitcast(U32).indirect(
                    offs_sb[:, lo // GROUP:(lo + length) // GROUP]))

        wa_pieces = [(0, 0, PASS)]
        for half, g in ((0, 1), (1, 0), (1, 1)):
            wa_pieces.extend((g, half * PASS + lo, PIECE) for lo in range(0, PASS, PIECE))
        wa_pieces = wa_pieces[:-1] + [(PASSES - 1, H - PIECE + lo, PIECE // 2) for lo in (0, PIECE // 2)]
        wa_raw = {}
        for g, lo, width in wa_pieces:
            shape, name = [P, PACK, width], "wa_raw%d_%d" % (g, lo)
            wa_raw[g, lo] = placed(shape, F32, name, LAST_PIECE) if lo + width == H and g == PASSES - 1 \
                else held(shape, F32, name)
            piece = wa[g * PASS:(g + 1) * PASS, lo:lo + width]
            nc.sync.dma_start(wa_raw[g, lo][:], piece.rearrange("(p i) c -> p i c", i=PACK))

        nc.sync.dma_start(sens_sb[:], sens.rearrange("(half m t) -> m half t", half=HALVES, t=PACK))
        wc_sb = [held([P, PASSES, PASS], I32, "wc_sb%d" % half) for half in range(HALVES)]

        def load_wc(half):
            words = wc_words.rearrange("g p c i -> p g (c i)")[:, :, half * PASS * PACK:(half + 1) * PASS * PACK]
            nc.sync.dma_start(wc_sb[half][:], words.bitcast(I32))

        pages = [held([P, T2], F32, "page%d" % n) for n in range(HALVES * PACK)]
        for n, page in enumerate(pages):
            if n < VECTOR_PAGES:
                clear_on_vector(page[:].bitcast(I32))
            else:
                nc.gpsimd.memset(page[:].bitcast(I32), 0)

        load_wc(0)
        wc_plane = held([P, PASSES, H], U8, "wc_plane")
        nc.gpsimd.memset(wc_plane[:].bitcast(I32), 0)
        load_plane(wc_plane, wc_scales)
        load_wc(1)
        wgo_sb = held([P, S], F32, "wgo_sb")
        nc.sync.dma_start(wgo_sb[:], wgo)
        nc.sync.dma_start(offs2_sb[:], offs2)

        wa_codes, wa_plane, wa_grouped = {}, {}, {}
        for half in range(HALVES):
            for g in range(PASSES):
                wa_codes[g, half] = held([P, PASS], U32, "wa_codes%d%d" % (g, half))
                wa_plane[g, half] = held([P, PASS], U8, "wa_plane%d%d" % (g, half))
        def round_wa(copy, g, lo, first, end):
            half, column = divmod(lo, PASS)
            to = wa_grouped[g, half][:, column + first:column + end, :].rearrange("p (c e) i -> p c i e", e=LINE)
            copy(to, wa_raw[g, lo][:, :, first:end].rearrange("p i (c e) -> p c i e", e=LINE))

        def round_on_scalar(to, source):
            nc.scalar.activation(to, source, ACT.Copy)

        def quantise_wa(g, half, first, end):
            nc.vector.quantize_mx(out=wa_codes[g, half][:, first:end].bitcast(FP8X4),
                                  scales=wa_plane[g, half][:, first:end],
                                  in_=wa_grouped[g, half][:, first:end, :].rearrange("p c i -> p (c i)"))

        for g, lo, width in wa_pieces:
            half, column = divmod(lo, PASS)
            if column == 0:
                wa_grouped[g, half] = held([P, PASS, PACK], BF16, "wa_grouped%d%d" % (g, half))
            on_scalar = (g, lo) == SCALAR_PIECE
            run = width if on_scalar else RUN[width]
            for first in range(0, width, run):
                round_wa(round_on_scalar if on_scalar else nc.vector.tensor_copy, g, lo, first, first + run)
            for first, end in QRUNS[g, lo]:
                quantise_wa(g, half, first, end)

        h_codes, h_plane = {}, {}

        def entries(q):
            return slice(q * P, (q + 1) * P)

        def channels(half):
            return slice(half * PASS, (half + 1) * PASS)

        def v_operand(q):
            return lambda g: (v_codes[g][:, entries(q)].bitcast(FP8X4), v_plane[:, g, entries(q)])

        def h_operand(q):
            return lambda g: (h_codes[q, g][:].bitcast(FP8X4), h_plane[q, g][:])

        def wa_operand(half, columns=slice(0, PASS)):
            return lambda g: (wa_codes[g, half][:, columns].bitcast(FP8X4), wa_plane[g, half][:, columns])

        def wb_operand(half):
            return lambda g: (wb_sb[:, g, 2 * PASS * half:2 * PASS * (half + 1)].bitcast(FP4X4),
                              wb_plane[:, g, channels(half)])

        def wc_operand(half):
            return lambda g: (wc_sb[half][:, g, :].bitcast(FP8X4), wc_plane[:, g, channels(half)])

        banks = [psum.tile([P, PASS], F32, name="bank%d" % n) for n in range(BANKS)]
        bank_of = {}

        def take(step, after):
            bank_of[step] = bank_of[after]
            return bank_of[step]

        def product(into, stationary, moving, order):
            for g in order:
                (lhs, lhs_scale), (rhs, rhs_scale) = stationary(g), moving(g)
                nc.tensor.matmul_mx(out=into, lhsT=lhs, lhsT_scale=lhs_scale, rhs=rhs, rhs_scale=rhs_scale,
                                    start=(g == order[0]), stop=(g == order[-1]))
            return into.rearrange("p (m t) -> p t m", t=PACK)

        def by_pairs(tile):
            return tile[:]

        def transposed_sum(bank, first, second):
            count = first.shape[1]
            total = bank[:, 0:count * P].rearrange("m (t j) -> m t j", t=count)
            for n, term in enumerate((first, second)):
                for t in range(count):
                    nc.tensor.matmul(total[:, t, :], lhsT=term[:, t, :], rhs=ident[:], is_transpose=True,
                                     start=(n == 0 and t == 0), stop=(n == 1 and t == count - 1))
            return total

        for n in range(WARM_UPS):
            nc.tensor.matmul_mx(out=banks[-1][:], lhsT=wb_sb[:, 0, 0:2 * P].bitcast(FP4X4),
                                lhsT_scale=wb_plane[:, 0, 0:P], rhs=word_window[0][:, 0:PASS].bitcast(FP8X4),
                                rhs_scale=wb_plane[:, 0, 0:PASS], start=True, stop=True)

        a_sb, minus_b = {}, {}

        def make_minus_b(q, half):
            bank = banks[len(minus_b)]
            bank_of["b%d%d" % (q, half)] = bank
            minus_b[q, half] = held([P, PACK, P], F32, "minus_b%d%d" % (q, half))
            b = product(bank[:], v_operand(q), wb_operand(half), FIRST_PASS_FIRST)
            if len(minus_b) in B_ON_VECTOR:
                nc.vector.tensor_scalar(by_pairs(minus_b[q, half]), b, -1.0, None, ALU.mult)
            else:
                nc.scalar.activation(by_pairs(minus_b[q, half]), b, ACT.Copy, scale=-1.0)

        def make_a(q, half, after, steps=((0, 0, PASS), (1, 0, PASS)), copy=nc.scalar.copy, place=None):
            if (q, half) not in a_sb:
                name = "a_sb%d%d" % (q, half)
                a_sb[q, half] = held([P, PACK, P], F32, name) if place is None \
                    else placed([P, PACK, P], F32, name, place)
            lo, hi = min(step[1] for step in steps), max(step[2] for step in steps)
            bank = take("a%d%d%s" % (q, half, "_%d" % lo if lo else ""), after)
            for g, first, end in steps:
                lhs, lhs_scale = v_operand(q)(g)
                rhs, rhs_scale = wa_operand(half, slice(first, end))(g)
                nc.tensor.matmul_mx(out=bank[:, first - lo:end - lo], lhsT=lhs, lhsT_scale=lhs_scale, rhs=rhs,
                                    rhs_scale=rhs_scale, start=((g, first, end) == steps[0]),
                                    stop=((g, first, end) == steps[-1]))
            a = bank[:, 0:hi - lo].rearrange("p (m t) -> p t m", t=PACK)
            copy(a_sb[q, half][:, :, lo // PACK:hi // PACK], a)

        def difference(q, half, after, b_first):
            terms = (minus_b[q, half], a_sb[q, half]) if b_first else (a_sb[q, half], minus_b[q, half])
            return transposed_sum(take("h%d%d" % (q, half), after), *terms)

        def quantise_h(q, half, h, parts=1):
            h_codes[q, half] = held([P, P], U32, "h_codes%d%d" % (q, half))
            h_plane[q, half] = held([P, P], U8, "h_plane%d%d" % (q, half))
            for lo in range(0, P, P // parts):
                run = slice(lo, lo + P // parts)
                nc.vector.quantize_mx(out=h_codes[q, half][:, run].bitcast(FP8X4), scales=h_plane[q, half][:, run],
                                      in_=h[:, run, :].rearrange("m j t -> m (j t)"))

        sizes = {}

        def make_size(q, half, after, parts=1):
            total = difference(q, half, after, True).rearrange("m t j -> m j t")
            sizes[q, half] = held([P, P, PACK], F32, "size%d%d" % (q, half))
            for lo in range(0, P, P // parts):
                run = slice(lo, lo + P // parts)
                nc.scalar.activation(sizes[q, half][:, run, :], total[:, run, :], ACT.Abs)

        def scale_on_vector(q, half, parts=1, place=None):
            h = passing([P, P, PACK], BF16, "h") if place is None \
                else placed([P, P, PACK], BF16, "h%d%d" % (q, half), place)
            factor = sens_sb[:, half:half + 1, :].to_broadcast([P, P // parts, PACK])
            for lo in range(0, P, P // parts):
                run = slice(lo, lo + P // parts)
                nc.vector.tensor_tensor(h[:, run, :], sizes[q, half][:, run, :], factor, ALU.mult)
            quantise_h(q, half, h, min(parts, QPARTS))

        def scale_on_scalar(q, half, after, place=None):
            total = difference(q, half, after, False)
            size = passing([P, PACK, P], F32, "size")
            nc.scalar.activation(size[:], total, ACT.Abs)
            h_rows = passing([P, PACK, P], BF16, "h_rows") if place is None \
                else placed([P, PACK, P], BF16, "h_rows%d%d" % (q, half), place)
            for t in range(PACK):
                nc.scalar.activation(h_rows[:, t, :], size[:, t, :], ACT.Copy, scale=sens_sb[:, half, t:t + 1])
            h = passing([P, P, PACK], BF16, "h")
            nc.scalar.copy(h[:].rearrange("m (c e) t -> m c t e", e=LINE),
                           h_rows[:].rearrange("m t (c e) -> m c t e", e=LINE))
            return h

        def make_y(q, half, into, c_after, y_after, order=LAST_PASS_FIRST, a_first=False, place=None):
            c_sb = passing([P, PACK, P], F32, "c_sb") if place is None \
                else placed([P, PACK, P], F32, "c_sb%d%d" % (q, half), place)
            c = product(take("c%d%d" % (q, half), c_after)[:], h_operand(q), wc_operand(half), order)
            nc.scalar.copy(by_pairs(c_sb), c)
            terms = (a_sb[q, half], c_sb) if a_first else (c_sb, a_sb[q, half])
            total = transposed_sum(take("y%d%d" % (q, half), y_after), *terms)
            lo = 0
            for part in into:
                nc.scalar.activation(part, total[:, lo:lo + part.shape[1], :], ACT.Tanh)
                lo = lo + part.shape[1]

        def make_y_by_pairs(q, half, into, c_after, y_after, a_first=(True, True), rows=((0, 2), (2, 4)), place=None):
            c_sb = passing([P, PACK, P], F32, "c_sb") if place is None \
                else placed([P, PACK, P], F32, "c_sb%d%d" % (q, half), place)
            bank = take("c%d%d" % (q, half), c_after)
            product(bank[:], h_operand(q), wc_operand(half), FIRST_PASS_FIRST)
            c = bank[:].rearrange("p (m t) -> p t m", t=PACK)
            for lo, hi in rows:
                nc.scalar.copy(c_sb[:, lo:hi, :], c[:, lo:hi, :])
            for u, (lo, hi) in enumerate(rows):
                bank = take("y%d%d_%d" % (q, half, u), y_after[u])
                terms = (a_sb[q, half][:, lo:hi, :], c_sb[:, lo:hi, :])
                total = transposed_sum(bank, *(terms if a_first[u] else terms[::-1]))
                nc.scalar.activation(into[:, lo:hi, :], total, ACT.Tanh)


        def scatter(y, q, half, rows=range(PACK)):
            lo, hi = q * P, q * P + y.shape[2]
            out_rows = out[channels(half), :].rearrange("(m t) s -> m t s", t=PACK)
            for n, t in enumerate(rows):
                page = pages[half * PACK + t]
                nc.vector.tensor_tensor(page[:].indirect(offs2_sb[:, lo // GROUP:hi // GROUP]),
                                        y[:, n, :], wgo_sb[:, lo:hi], ALU.mult)
                if hi == S:
                    nc.sync.dma_start(out_rows[:, t, :], page[:])

        def y_tile(q, half, quarters=1):
            return held([P, PACK, quarters * P], F32, "y%d%d" % (q, half))

        for q, half in ((0, 0), (1, 0), (3, 0), (2, 1), (0, 1), (1, 1), (2, 0), (3, 1)):
            make_minus_b(q, half)
        y00, y01, y30 = y_tile(0, 0), y_tile(0, 1), y_tile(3, 0)
        last = PASS - PIECE // 2
        by_pieces = ((0, 0, PASS), (1, 0, PIECE), (1, PIECE, PASS))

        make_a(0, 0, after="b30")
        make_size(0, 0, after="b00")
        scale_on_vector(0, 0, place=H00)
        make_a(1, 0, after="b21")
        make_size(1, 0, after="b10")
        make_a(0, 1, after="b31", steps=((0, 0, PIECE), (0, PIECE, last), (1, 0, PIECE), (1, PIECE, last)))
        make_a(0, 1, after="h00", steps=((0, last, PASS), (1, last, PASS)))
        make_size(0, 1, after="b01", parts=HPARTS)
        scale_on_vector(0, 1, parts=HPARTS, place=H01)
        make_a(1, 1, after="a10", steps=by_pieces)
        make_a(2, 0, after="a00", copy=nc.vector.tensor_copy, place=A20)
        scale_on_vector(1, 0, place=H10)
        make_size(2, 0, after="b20")
        make_size(1, 1, after="b11")
        make_y_by_pairs(0, 0, y00, c_after="a01", y_after=("a01_384", "a20"), rows=ROWS, place=C0)
        scale_on_vector(2, 0)
        scale_on_vector(1, 1)
        make_a(2, 1, after="h10", steps=((1, 0, PASS), (0, 0, PASS)), copy=nc.vector.tensor_copy, place=H01)
        make_a(3, 0, after="h01")
        scatter(y00, 0, 0)
        make_y(0, 1, [y01[:]], c_after="a11", y_after="y00_0", a_first=True, order=FIRST_PASS_FIRST, place=C0)
        scatter(y01, 0, 1)

        def late(q, half, after, n, y_name, rows=PACK):
            place = LATE_ROWS + n * 2 * KIB
            quantise_h(q, half, scale_on_scalar(q, half, after=after, place=place))
            return placed([P, rows, P], F32, y_name, place)

        y10 = late(2, 1, "c00", 0, "y10", PACK - 1)
        y10_first = held([P, 1, P], F32, "y10_first")
        make_y(1, 0, [y10_first[:], y10[:]], c_after="y00_1", y_after="y01", order=FIRST_PASS_FIRST, a_first=True)
        scatter(y10_first, 1, 0, range(1))
        scatter(y10, 1, 0, range(1, PACK))
        y11 = late(3, 0, "h21", 1, "y11", PACK - 1)
        y11_first = held([P, 1, P], F32, "y11_first")
        make_y(1, 1, [y11_first[:], y11[:]], c_after="c10", y_after="h11")
        scatter(y11_first, 1, 1, range(1))
        scatter(y11, 1, 1, range(1, PACK))
        make_a(3, 1, after="c01")
        y20 = late(3, 1, "h30", 2, "y20")
        make_y(2, 0, [y20[:]], c_after="y10", y_after="a31", order=FIRST_PASS_FIRST, a_first=True)
        scatter(y20, 2, 0)
        make_y_by_pairs(3, 0, y30, c_after="h31", y_after=("y11", "c11"))
        scatter(y30, 3, 0)
        y21 = y_tile(2, 1, quarters=2)
        make_y(2, 1, [y21[:, :, entries(0)]], c_after="c20", y_after="h20")
        make_y(3, 1, [y21[:, :, entries(1)]], c_after="y20", y_after="a30")
        scatter(y21, 2, 1)
